import numpy as np, ml_dtypes
CORES = [40,41,42,43,44,45,46,47]
N = 8
import mx_ref
BF = ml_dtypes.bfloat16
def gentries(a):
    return np.ascontiguousarray(a.reshape(8, 16, -1).transpose(0, 2, 1)).reshape(8, -1)
def gtable(e):
    e = np.asarray(e); return np.ascontiguousarray(e.reshape(8, -1, 16).transpose(0, 2, 1)).reshape(128, -1).astype(np.int32)
def gcols(t, e):
    v = np.concatenate([t.reshape(8, 16, -1, 4), np.zeros((8, 16, 1, 4), BF)], axis=2)
    return np.ascontiguousarray(np.stack([v[g][:, e[g]] for g in range(8)])).reshape(128, -1)
def tile(rs):
    return np.stack(rs, axis=2).reshape(128, -1).astype(BF)
def pick(q, e):
    c = np.concatenate([q[0].reshape(128, -1, 4), np.zeros((128, 1, 4), np.uint8)], axis=1); s = np.concatenate([q[1], np.ones((16, 1), np.uint8)], axis=1)
    return (np.ascontiguousarray(c[:, e].reshape(128, -1)), np.ascontiguousarray(s[:, e]))
def join(*qs):
    return (np.concatenate([q[0] for q in qs], axis=1), np.concatenate([q[1] for q in qs], axis=1))
def put(q, e, v):
    c, s = q[0].reshape(128, -1, 4).copy(), q[1].copy(); c[:, e] = v[0].reshape(128, -1, 4); s[:, e] = v[1]
    return (c.reshape(128, -1), s)
def pk(c, s):
    return (np.ascontiguousarray(c), mx_ref.live(s))
def emit(q):
    return q[0], q[1]
def packed(v, rng):
    q = [mx_ref.quantize(np.ascontiguousarray(v[r])) for r in range(N)]
    return np.stack([a for a, b in q]), np.stack([mx_ref.plane(b, rng) for a, b in q])
def values_of_codes():
    e, c = np.zeros((128, 128, 4), np.float32), np.zeros((128, 2, 4), np.uint8)
    e[np.arange(128), np.arange(128), 0] = 1
    c[:127, :, 0] = np.arange(256).reshape(2, 128).T[:127]
    return mx_ref.matmul(mx_ref.quantize(e.reshape(128, 512).astype(BF)), (c.reshape(128, 8), np.full((16, 2), 127, np.uint8))).T.reshape(-1).astype(np.float64)
CODE_VALUE, SCALE_VALUE = values_of_codes(), 2.0 ** (np.arange(256) - 127.0)
def decode(q):
    return (CODE_VALUE[q[0]].reshape(16, 8, -1, 4) * SCALE_VALUE[q[1]][:, None, :, None] + 0.0).reshape(128, -1).astype(np.float32)
def f(rng, *shape):
    return mx_ref.flush((rng.standard_normal(shape, dtype=np.float32) * np.exp2(rng.integers(-2, 3, shape[:-1] + (1,)))).astype(BF))
def wide(rng, *shape, cols=0):
    v = rng.standard_normal(shape, dtype=np.float32) * np.exp2(rng.integers(-12, 13, shape)).astype(np.float32)
    if cols: v *= np.repeat(np.exp2(rng.integers(-cols, cols + 1, shape[:-2] + (1, shape[-1] // 4))) * (rng.random(shape[:-2] + (1, shape[-1] // 4)) > 0.0625), 4, axis=-1).astype(np.float32)
    return mx_ref.flush(v.astype(BF))
C, H, R = 320, 128, 3
def big(v):
    v = v.astype(np.float32)
    v[np.abs(v) < np.float32(2.0 ** -16)] = 0
    return v.astype(BF)
def numbers_of(rng):
    return {"x": big(f(rng, N, 128, 4 * C)), "u": np.array(f(rng, N, 128, 512)), "v": np.array(f(rng, N, 128, 512))}
def layers(rng, still=[]):
    w = big(f(rng, N, 128, 2048)).reshape(N, 8, 16, 4, 8, 16, 4)
    for i in still: w[:, :, :, :, :, i] = 0
    return w
def weights(rng, w):
    c, s = packed(np.ascontiguousarray(w).reshape(N, 128, 2048), rng)
    return {"wc": c, "ws": s}
def holes(rng):
    return np.sort(np.argsort(rng.random((N, 8, C - 1)), axis=2)[:, :, :H], axis=2)
def throws(rng, a):
    free = np.ones((N, 8, 2 * C), bool)
    free[:, :, C:] = False
    np.put_along_axis(free, a, False, axis=2)
    np.put_along_axis(free, C + np.roll(a, -1, axis=0), True, axis=2)
    e = np.zeros((N, 8, C), np.int64)
    for i in range(C - 1, -1, -1):
        k = (0.5 + rng.random((N, 8, C))) * free[:, :, i:i + C]
        k[:, :, C - 1] = 2.0 * free[:, :, i + C - 1]
        e[:, :, i] = i + np.argmax(k, axis=2)
        np.put_along_axis(free, e[:, :, i:i + 1], False, axis=2)
    return e
def lists(e):
    return np.stack([gtable(e[r]) for r in range(N)])
def meet(rng, e):
    used, out = [False] * C, []
    e = e.tolist()
    for i, k in zip(rng.permutation(C).tolist(), rng.integers(0, 4, C).tolist()):
        j = e[i] + (0, 1, 1 - C, -C)[k]
        if 0 <= j < C and j != i and not used[i] and not used[j]:
            used[i] = used[j] = True
            out += [i, j]
    return np.array(out + [int(i) for i in rng.permutation(C) if not used[i]])
def setup_inputs(rng):
    return {**numbers_of(rng), "p": lists(throws(rng, holes(rng))), **weights(rng, layers(rng))}
def setup_inputs_ties(rng):
    d = numbers_of(rng)
    o = rng.permutation(N)
    x = d["x"].reshape(N, 8, 16, C, 4)
    k = rng.integers(0, 3, (N, 8, C))
    k[o[2]] = 1
    x[:, :, 0] = 0
    x[:, :, 0, :, 0] = k.astype(np.float32).astype(BF)
    u = d["u"].reshape(N, 128, 128, 4)
    u[:, :, ::16] = 0
    for r in range(N):
        for h in range(0, 128, 16): u[r, h, h, 0] = 0.0 if r == o[0] else -1.0 if r == o[1] else 1.0
    return {"x": x.reshape(N, 128, 4 * C), "u": u.reshape(N, 128, 512), "v": d["v"], "p": lists(throws(rng, holes(rng))), **weights(rng, layers(rng, [0]))}
def setup_inputs_near(rng):
    d = numbers_of(rng)
    o = rng.permutation(N) % 4
    low = rng.permutation(8)[:4]
    x = d["x"].astype(np.float32).reshape(N, 8, 16, C, 4)
    u = d["u"].reshape(N, 128, 128, 4)
    x[:, :, 0] = 0
    x[:, :, 8:] = 0
    u[:, :, ::16] = 0
    for r in range(N):
        k = 1.0 if o[r] == 0 else 2.0 ** -30
        if o[r] < 3:
            s = rng.integers(0, 16, (8, C))
            x[r, :, 8] = ((s[:, :, None] >> np.arange(4)) & 1) * np.exp2(np.arange(4) - 23.0)
        else:
            x[r, :, 8, :, 0] = rng.integers(8, 16, (8, C)) * rng.choice([-1.0, 1.0], (8, C)) * 2.0 ** -27
            for g in low: x[r, g, 8:10, :, 0] = rng.integers(8, 15, (2, C)) * 2.0 ** -30
        if o[r] < 2:
            x[r, :, 0, :, 0] = rng.choice([-1.0, 1.0], (8, C))
            x[r, :, 11, :, 0] = 2.0 ** -10
        if o[r] == 2:
            for g in rng.permutation(8)[:4]: x[r, g, 0, rng.integers(C), 0] = 2.0 ** 29
        for h in range(0, 128, 16):
            u[r, h + 8, h] = k
            if o[r] < 2:
                u[r, h, h, 0] = k
                u[r, h + 11, h, 0] = k
            if o[r] == 2: u[r, h, h, 0] = 1.0
            if o[r] == 3 and h // 16 in low: u[r, h + 9, h] = -k
    still = [0, 8, 9, 10, 11, 12, 13, 14, 15]
    w = layers(rng, still)
    w[:, :, still] = 0
    return {"x": x.reshape(N, 128, 4 * C).astype(BF), "u": u.reshape(N, 128, 512), "v": d["v"], "p": lists(throws(rng, holes(rng))), **weights(rng, w)}
def setup_inputs_huge(rng):
    d = numbers_of(rng)
    h, o = rng.permutation(8), rng.permutation(N)
    c = rng.choice([-1.0, 1.0], (N, 1, 1, C, 1))
    c[o == 0] = 1.0
    x = (0.9 + 0.1 * rng.random((N, 8, 16, C, 4))) * 2.0 ** 30
    x[:, h[4:]] *= c
    a = (0.9 + 0.1 * rng.random((N, 8, 16, 8, 4))) * 2.0 ** 30
    for r in range(N):
        if o[r] == 0: a[r] *= -1.0
        elif o[r] % 2 == 1:
            a[r] *= -1.0
            a[r, h[4:]] = 0
        else: a[r, h[:4]] = 0
    u = d["u"].reshape(N, 128, 128, 4)
    u[:, :, ::16] = a.reshape(N, 128, 8, 4).astype(np.float32).astype(BF)
    w = np.zeros((N, 128, 4, 128, 4), np.float32)
    i = np.arange(128)
    for b in range(4): w[:, i, b, i, b] = -1
    return {"x": x.astype(np.float32).reshape(N, 128, 4 * C).astype(BF), "u": u.reshape(N, 128, 512), "v": d["v"], "p": lists(throws(rng, holes(rng))), **weights(rng, w.astype(BF))}
def setup_inputs_edges(rng):
    d = numbers_of(rng)
    h, a = rng.permutation(8), holes(rng)
    a[:, h[:2]] = np.arange(H)
    a[:, h[2:4]] = np.arange(C - 1 - H, C - 1)
    e = throws(rng, a)
    e[:, h[:2]] = np.arange(C) + H
    x = d["x"].reshape(N, 8, 16, C, 4)
    x[:, :, :3] = 0
    for r in range(N):
        for g in range(8):
            n = np.zeros(C, np.int64)
            n[meet(rng, e[r, g])] = np.arange(C - 1, -1, -1)
            for i in range(3): x[r, g, i, :, 0] = ((n >> (6 - 3 * i)) & 7).astype(np.float32).astype(BF)
    k = np.exp2(rng.integers(-2, 3, (N, 8, 1, C, 1)))
    b = (2 * rng.integers(0, 8, (N, 8, 8, C, 4)) + 1) * 2.0 ** -16 * k
    b[:, :, 0, :, 0] = 1.96875 * k[:, :, 0, :, 0]
    b *= rng.choice([-1.0, 1.0], b.shape)
    x[:, :, 8:] = b.astype(np.float32).astype(BF)
    u = d["u"].reshape(N, 128, 128, 4)
    u[:, :, ::16] = 0
    for g in range(0, 128, 16):
        for i in range(3): u[:, g + i, g, 0] = 2.0 ** (6 - 3 * i)
    return {"x": x.reshape(N, 128, 4 * C), "u": u.reshape(N, 128, 512), "v": d["v"], "p": lists(e), **weights(rng, layers(rng, [0, 1, 2, 8, 9, 10, 11, 12, 13, 14, 15]))}
def setup_inputs_spread(rng):
    d = setup_inputs(rng)
    d["x"] = big(wide(rng, N, 128, 4 * C, cols=6))
    return d
def check_inputs(d):
    b = []
    for k in ("x", "u", "v"):
        a = np.abs(d[k].astype(np.float32))
        if not (np.isfinite(a).all() and ((a == 0) | (a >= 2.0 ** -30) & (a <= 2.0 ** 30)).all()): b.append("a value of " + k)
    e = np.stack([gentries(d["p"][r]) for r in range(N)]).astype(np.int64)
    t, s = e - np.arange(C), np.sort(e, axis=2)
    if ((t < 0) | (t >= C)).any(): b.append("p: a landing out of its column's bounds")
    if (s[:, :, 1:] == s[:, :, :-1]).any(): b.append("p: equal landings")
    if (np.count_nonzero(e >= C, axis=2) != H).any(): b.append("p: the number of crossing landings")
    k = np.concatenate([s[:, :, :C - H], np.roll(s[:, :, C - H:], 1, axis=0) - C], axis=2)
    if (np.sort(k, axis=2) != np.arange(C)).any(): b.append("p: crossing landings aren't the next rank's holes")
    none, least, most = [emit(mx_ref.quantize(np.full((128, 16), k, np.float32).astype(BF)))[1][0, 0] for k in (0.0, 2.0 ** -30, 2.0 ** 30)]
    for r in range(N):
        if ((d["wc"][r] == 0x7F) | (d["wc"][r] == 0xFF)).any(): b.append("wc: a code that is no number")
        s = mx_ref.live(d["ws"][r])
        if ((s != none) & ((s < least) | (s > most))).any(): b.append("ws: a scale out of range")
    return b
def reference(x, u, v, p, wc, ws):
    qu = [mx_ref.quantize(u[r]) for r in range(N)]
    lay = [pk(wc[r], ws[r]) for r in range(N)]
    now = [x[r] for r in range(N)]
    land = np.stack([gentries(p[r]) for r in range(N)]).astype(np.int64)
    for t in range(R):
        for r in range(N):
            s = mx_ref.matmul(qu[r], mx_ref.quantize(now[r]))[::16] + np.float32(0.0)
            o = np.argsort(-s, axis=1, kind="stable")
            a, b = o[:, ::2], o[:, 1::2]
            la, lb = np.take_along_axis(land[r], a, axis=1), np.take_along_axis(land[r], b, axis=1)
            ok = (a <= lb) & (lb < a + C) & (b <= la) & (la < b + C)
            np.put_along_axis(land[r], a, np.where(ok, lb, la), axis=1)
            np.put_along_axis(land[r], b, np.where(ok, la, lb), axis=1)
        back, hits = np.argsort(land, axis=2), np.sort(land, axis=2)
        given = [mx_ref.quantize(gcols(now[r], back[r][:, C - H:])) for r in range(N)]
        new = []
        for r in range(N):
            both = np.concatenate([now[r], decode(given[r - 1]).astype(BF)], axis=1)
            e = np.zeros((8, C), np.int64)
            np.put_along_axis(e, hits[r][:, :C - H], back[r][:, :C - H], axis=1)
            np.put_along_axis(e, hits[r - 1][:, C - H:] - C, np.stack([C + np.arange(H)] * 8), axis=1)
            z = ((gcols(both, e).astype(np.float32) + now[r].astype(np.float32)) * np.float32(0.5)).astype(BF)
            q = mx_ref.quantize(z)
            new.append(tile([mx_ref.matmul(pick(lay[r], np.arange(128 * b, 128 * b + 128)), q) * np.float32(0.03125) + z[:, b::4].astype(np.float32) for b in range(4)]))
        now = new
    y, ol = np.zeros((N, 128, C), np.float32), np.zeros((N, 8, C), np.float32)
    oc, osc = np.zeros((N, 128, 4 * C), np.uint8), np.zeros((N, 16, C), np.uint8)
    for r in range(N):
        q = mx_ref.quantize(now[r])
        y[r] = mx_ref.matmul(mx_ref.quantize(v[r]), q)
        ol[r] = land[r]
        oc[r], osc[r] = emit(q)
    return {"y": y, "ol": ol, "oc": oc, "osc": osc}

@@ -1,0 +1,354 @@
+from concourse.mybir import dt, AluOpType, ActivationFunctionType, AxisListType
+
+A = AluOpType
+COPY = ActivationFunctionType.Copy
+C, ROUNDS = 320, 3
+E = C + 32
+M = C // 2
+NC = C // 16
+F8 = "float8_e4m3fn_x4"
+
+SCRATCH = {}
+
+
+def _declare(names, columns, dtype, where="sbuf"):
+    for name in names.split():
+        SCRATCH[name] = (where, [128, columns], dtype)
+
+
+_declare("xt0 xt1", 4 * E, "bfloat16")
+_declare("z z32 uu hx", 4 * C, "bfloat16")
+_declare("ut vt", 512, "bfloat16")
+_declare("eo ee", 516, "bfloat16")
+_declare("hw", 8 * C, "bfloat16")
+_declare("fb", NC * C, "bfloat16")
+_declare("te ts kk", C, "bfloat16")
+_declare("uq uqr vq", 128, F8)
+_declare("us usr vs", 128, "uint8")
+_declare("wq eq", 512, F8)
+_declare("wp es", 512, "uint8")
+_declare("zq qx3 qp0 qp1 qp2", C, F8)
+_declare("zs sx3 sp0 sp1 sp2", C, "uint8")
+_declare("qx0 qx1 qx2", E, F8)
+_declare("sx0 sx1 sx2", E, "uint8")
+_declare("gb", E, "float32")
+_declare("wb", 3 * C, "float32")
+_declare("tt", C + E, "float32")
+_declare("nb ex vb wo j16 iof iog iov yb olb l50 l51 l52", C, "float32")
+_declare("sw qa qb ka kb", 32, "float32")
+_declare("acc pq pxi xb ca cb oa ob dl ls m1 md mm e5 f1 db pm pf ci iw pbf lw0 lw1 lw2 lw3", NC, "float32")
+_declare("qf q20 k1 k2 k3", 1, "float32")
+_declare("pli hh pin", NC, "int32")
+_declare("bl", 32, "int32")
+_declare("pb", C, "int32")
+_declare("c8", 8, "int32")
+_declare("pi qi oi si ri", 1, "int32")
+_declare("plu pxu pu exl pbl lu0 lu1 lu2 la0 la1 la2", NC, "uint16")
+_declare("eu", 32, "uint16")
+_declare("ul", 8, "uint16")
+_declare("wl", 2, "uint16")
+_declare("ps0 ps1 ps2 ps3 ps4 ps5 ps6 ps7", 512, "float32", "psum")
+
+SEMAPHORES = (["v", "a", "t", "gc_", "dx", "du", "dp", "dpb", "dw", "dv", "dy", "dol", "doc"]
+              + ["%s%d" % (n, t) for n in ("rq", "rl", "lq", "ll") for t in range(ROUNDS)])
+
+
+def rank_program(g, core, T, topo):
+    rank = T.rank_of(core)
+    if rank is None:
+        return
+    nxt = T.cores[(rank + 1) % len(T.cores)]
+    rid, pid = topo.addr(nxt)[:2]
+    mask = topo.mask(core, nxt)
+    nmask = len(topo.engines(core, nxt))
+    eng = {"v": g.vector, "a": g.scalar, "t": g.tensor, "gc_": g, "s": g.sync}
+
+    count, known, snap = {}, {q: {} for q in eng}, {}
+    wrote, read, order = {}, {}, [0]
+
+    def need(q, toks):
+        for k in sorted(set(toks), key=lambda k: (snap.get(k, (0, {}))[0], k), reverse=True):
+            if known[q].get(k[0], 0) >= k[1]:
+                continue
+            eng[q].wait_ge(T.sem[k[0]], k[1])
+            for s, m in list(snap.get(k, (0, {}))[1].items()) + [k]:
+                if known[q].get(s, 0) < m:
+                    known[q][s] = m
+
+    def deps(q, reads, writes):
+        toks = []
+        for k in reads:
+            if k in wrote:
+                toks.append(wrote[k])
+            if k[:2] == "ps":
+                toks += [(s, m) for s, m in read.get(k, {}).items() if s != q]
+        for k in writes:
+            if k in wrote:
+                toks.append(wrote[k])
+            toks += [(s, m) for s, m in read.get(k, {}).items() if s != q]
+        return toks
+
+    def note(tok, reads, writes, q):
+        order[0] += 1
+        snap[tok] = (order[0], dict(known[q]))
+        for k in reads:
+            read.setdefault(k, {})[tok[0]] = tok[1]
+        for k in writes:
+            wrote[k] = tok
+            read[k] = {}
+
+    def op(q, fn, reads, writes):
+        need(q, deps(q, reads, writes))
+        fn().then_inc(T.sem[q], 1)
+        count[q] = count.get(q, 0) + 1
+        note((q, count[q]), reads, writes, q)
+
+    def dma(q, out, in_, sem, reads, writes):
+        need(q, deps(q, reads, writes))
+        eng[q].dma_start(out, in_).then_inc(T.sem[sem], 16)
+        count[sem] = count.get(sem, 0) + 16
+        note((sem, count[sem]), reads, writes, q)
+
+    def send(out, in_, rsem, lsem, reads):
+        need("gc_", deps("gc_", reads, []))
+        g.remote_dma(out, in_, T.sem[rsem], T.sem[lsem], pid, rid, mask)
+        count[lsem] = count.get(lsem, 0) + nmask
+
+    V, S, P = g.vector, g.scalar, g.tensor
+
+    def tt(out, a, b, o, reads, writes):
+        op("v", lambda: V.tensor_tensor(out, a, b, o), reads, writes)
+
+    def ts(out, a, s1, s2, o, reads, writes):
+        if len(o) == 1:
+            op("v", lambda: V.tensor_scalar(out, a, s1, None, o[0]), reads, writes)
+        else:
+            op("v", lambda: V.tensor_scalar(out, a, s1, s2, o[0], o[1]), reads, writes)
+
+    def cp(out, a, reads, writes):
+        op("v", lambda: V.tensor_copy(out, a), reads, writes)
+
+    def act(out, a, reads, writes, scale=1.0, accum=None):
+        op("a", lambda: S.activation(out, a, COPY, scale=scale, accum_out=accum), reads, writes)
+
+    def quant(q, s, a, reads, writes):
+        op("v", lambda: V.quantize_mx(q, s, a), reads, writes)
+
+    def mm(out, lq, ls, rq, rs, reads, writes):
+        op("t", lambda: P.matmul_mx(out, lq, ls, rq, rs, True, True), reads, writes)
+
+    for t in range(ROUNDS):
+        wrote["qp%d" % t] = ("rq%d" % t, 2 * nmask)
+        wrote["la%d" % t] = ("rl%d" % t, nmask)
+
+    lo, hi = 4 * 16, 4 * (16 + C)
+    dma("s", T.xt0[:, lo:hi], T.x[:], "dx", [], [])
+    dma("a", T.ut[:], T.u[:], "du", [], ["ut"])
+    dma("s", T.xt0[:, 0:lo], T.x[:, 0:lo], "dx", [], [])
+    dma("s", T.xt0[:, hi:hi + lo], T.x[:, 0:lo], "dx", [], ["xt"])
+    for r in range(16):
+        dma("a", T.pb[r:128:16, :], T.p[:], "dpb", [], [])
+    wrote["pb"] = ("dpb", count["dpb"])
+    dma("s", T.pin[:], T.p[:], "dp", [], ["pin"])
+    dma("s", T.wq[:].bitcast(dt.uint8), T.wc[:], "dw", [], [])
+    dma("s", T.wp[:], T.ws[:], "dw", [], ["w"])
+    dma("s", T.vt[:], T.v[:], "dv", [], ["vt"])
+
+    def iota(out, pattern, base, mul, key):
+        op("gc_", lambda: g.iota(out, pattern, base, mul, allow_small_or_imprecise_dtypes=True), [], [key])
+
+    op("v", lambda: V.memset(T.eo[:], 1.0), [], ["eo"])
+    for name, k, w in (("gb", 0, 16), ("gb", C + 16, 16), ("wb", C - 16, 16), ("wb", 2 * C, 16), ("ka", 20, 12), ("kb", 20, 12)):
+        op("v", lambda: V.memset(T[name][:, k:k + w], 0.0), [], ["%s_pad%d" % (name, k)])
+    wrote["gb_pad"], wrote["wb"] = wrote["gb_pad%d" % (C + 16)], wrote["wb_pad%d" % (2 * C)]
+    iota(T.c8[:], [[16, 8]], 0, 0, "c8")
+    iota(T.pi[:], [[1, 1]], 0, 1, "pi")
+    iota(T.ci[:], [[1, NC]], 0, 0, "ci")
+    iota(T.j16[:], [[0, NC], [1, 16]], 0, 0, "j16")
+    op("gc_", lambda: g.affine_select(T.ee[:], T.eo[:], [[1, 516]], A.is_equal, 0.0, -3, -4), ["eo"], ["ee"])
+    iota(T.iof[:], [[1, C]], 0, 0, "iof")
+    cp(T.ul[:], T.c8[:], ["c8"], ["ul"])
+    ts(T.qi[:], T.pi[:], 15, None, [A.bitwise_and], ["pi"], ["qi"])
+    ts(T.oi[:], T.pi[:], 16, 4, [A.bitwise_and, A.arith_shift_right], ["pi"], ["oi"])
+    cp(T.exl[:], T.ci[:], ["ci"], ["exl"])
+    cp(T.qf[:], T.qi[:], ["qi"], ["qf"])
+    tt(T.si[:], T.qi[:], T.oi[:], A.add, ["qi", "oi"], ["si"])
+    ts(T.k2[:], T.qi[:], 16.0, None, [A.mult], ["qi"], ["k2"])
+    ts(T.q20[:], T.qf[:], 20.0, None, [A.mult], ["qf"], ["q20"])
+    ts(T.ri[:], T.si[:], 1, None, [A.bitwise_and], ["si"], ["ri"])
+    ts(T.iw[:], T.ci[:], 16.0, T.qf[:, 0:1], [A.mult, A.add], ["ci", "qf"], ["iw"])
+    ts(T.k1[:], T.ri[:], float(C + 16), None, [A.mult], ["ri"], ["k1"])
+    ts(T.pbf[:], T.ci[:], T.q20[:, 0:1], None, [A.add], ["ci", "q20"], ["pbf"])
+    tt(T.k3[:], T.k1[:], T.k2[:], A.add, ["k1", "k2"], ["k3"])
+    cp(T.ka[:, 0:NC], T.iw[:], ["iw"], ["ka"])
+    cp(T.pbl[:], T.pbf[:], ["pbf"], ["pbl"])
+    cp(T.wl[:, 0:1], T.k3[:], ["k3"], ["wl0"])
+    ts(T.wl[:, 1:2], T.k3[:], 256.0, float(C + E - 1), [A.add, A.min], ["k3"], ["wl1"])
+    ts(T.kk[:], T.j16[:], T.qf[:, 0:1], None, [A.is_gt], ["j16", "qf"], ["kk"])
+
+    quant(T.uq[:], T.us[:], T.ut[:], ["ut"], ["uq"])
+    op("v", lambda: V.tensor_copy(T.uqr[:, 0:128].bitcast(dt.uint32), T.uq[:, 0:128].bitcast(dt.uint32).indirect(T.ul[:, 0:8])), ["uq", "ul"], ["uqr"])
+    op("v", lambda: V.tensor_copy(T.usr[:, 0:128], T.us[:, 0:128].indirect(T.ul[:, 0:8])), ["uq", "ul"], ["usr"])
+    for b in range(4):
+        quant(T.eq[:, 128 * b:128 * b + 128], T.es[:, 128 * b:128 * b + 128], T.ee[:, 3 - b:515 - b], ["ee"], ["eq%d" % b])
+
+    def turn(at, in_, keys, key):
+        w = in_.shape[1]
+        op("v", lambda: V.transpose(T.tt[:, at:at + w], in_), keys, [key])
+
+    turned = T.tt[:].indirect(T.wl[:])
+    wlk = ["wl0", "wl1"]
+
+    for t in range(ROUNDS):
+        xt = T.xt0 if t == 0 else T.xt1
+        qx, sx, qk = T["qx%d" % t], T["sx%d" % t], ["qx%d_0" % t, "qx%d_1" % t]
+        if t == 0:
+            quant(qx[:, 0:16 + M], sx[:, 0:16 + M], xt[:, 0:lo + 4 * M], ["xt"], qk[:1])
+            quant(qx[:, 16 + M:E], sx[:, 16 + M:E], xt[:, lo + 4 * M:4 * E], ["xt"], qk[1:])
+        else:
+            quant(qx[:, 0:16 + M], sx[:, 0:16 + M], xt[:, 0:lo + 4 * M], ["x%d_0" % b for b in range(4)] + ["xpad0"], qk[:1])
+            ts(xt[:, lo + 4 * M + 3:hi:4], T.uu[:, 3 * C + M:4 * C], 2.0 ** -5, None, [A.mult], ["uu3_1"], ["x3_1"])
+            quant(qx[:, 16 + M:E], sx[:, 16 + M:E], xt[:, lo + 4 * M:4 * E], ["x%d_1" % b for b in range(4)] + ["xpad1"], qk[1:])
+        uk = ["uqr", "usr"]
+        mm(T.ps6[:, 0:16 + M], T.uqr[:], T.usr[:], qx[:, 0:16 + M], sx[:, 0:16 + M], uk + qk[:1], ["ps6"])
+        mm(T.ps0[:, 0:M], T.uqr[:], T.usr[:], qx[:, 16:16 + M], sx[:, 16:16 + M], uk + qk[:1], ["ps0"])
+        mm(T.ps7[:, 0:32 + M], T.uqr[:], T.usr[:], qx[:, M:E], sx[:, M:E], uk + qk, ["ps7"])
+        mm(T.ps5[:, 0:M], T.uqr[:], T.usr[:], qx[:, 16 + M:16 + C], sx[:, 16 + M:16 + C], uk + qk[1:], ["ps5"])
+        send(T["qp%d" % t][:].bitcast(dt.uint8), qx[:, 16:16 + C].bitcast(dt.uint8), "rq%d" % t, "lq%d" % t, qk)
+        send(T["sp%d" % t][:], sx[:, 16:16 + C], "rq%d" % t, "lq%d" % t, qk)
+        act(T.nb[:, 0:M], T.ps0[:, 0:M], ["ps0"], ["nb0"])
+        act(T.nb[:, M:C], T.ps5[:, 0:M], ["ps5"], ["nb1"])
+        if t == 0:
+            iota(T.iog[:], [[1, C]], C, 0, "iog")
+            cp(T.l50[:], T.pb[:].indirect(T.pbl[:]), ["pb", "pbl"], ["l50"])
+        turn(0, T.ps6[:, 16:16 + M], ["ps6"], "ta0")
+        turn(C, T.ps6[:, 0:M], ["ps6"], "tb0")
+        turn(M, T.ps7[:, 16:16 + M], ["ps7"], "ta1")
+        turn(C + M, T.ps7[:, 0:32 + M], ["ps7"], "tb1")
+        tk = ["ta0", "tb0", "ta1", "tb1"]
+        cp(T.sw[:], turned, tk + wlk, ["sw"])
+        sk = ["nb0", "nb1", "sw"]
+        lw, ln, lk = T["lw%d" % t], T["lw%d" % (t + 1)], "lw%d" % t
+        for c in range(NC):
+            f, e, sc = C * c, 16 * c + 16, T.sw[:, c:c + 1]
+            fk = ["fl%d" % c, "fh%d" % c]
+            ts(T.fb[:, f:f + e], T.nb[:, 0:e], sc, None, [A.is_ge], sk, fk[:1])
+            if e < C:
+                ts(T.fb[:, f + e:f + C], T.nb[:, e:C], sc, None, [A.is_gt], sk, fk[1:])
+            if c == NC - 1:
+                op("v", lambda: V.tensor_reduce(T.acc[:, c:c + 1], T.fb[:, f:f + C], AxisListType.X, A.add), fk, ["acc%d" % c])
+            else:
+                act(T.fb[:, f:f + C], T.fb[:, f:f + C], fk, fk + ["acc%d" % c], accum=T.acc[:, c:c + 1])
+            if c == 4:
+                act(T.ex[:], T.sw[:].indirect(T.exl[:]), ["sw", "exl"], ["ex"])
+            if c == 8 and t == 0:
+                cp(T.lw0[:], T.pin[:], ["pin"], ["lw0"])
+                ts(T.iov[:], T.iof[:], float(-M), 2.0 ** -9, [A.add, A.mult], ["iof"], ["iov"])
+            if c == 10 and t == 0:
+                tt(T.vb[:], T.l50[:], T.iov[:], A.add, ["l50", "iov"], ["vb"])
+            if c == 15:
+                ts(T.kb[:, 0:NC], lw[:], float(-M), 2.0 ** -9, [A.add, A.mult], [lk], ["kb"])
+                tt(T.f1[:], lw[:], T.iw[:], A.subtract, [lk, "iw"], ["f1"])
+            if c == 16:
+                tt(T.te[:, 0:M], T.ps0[:, 0:M], T.ex[:, 0:M], A.is_equal, ["ps0", "ex"], ["te0"])
+                tt(T.te[:, M:C], T.ps5[:, 0:M], T.ex[:, M:C], A.is_equal, ["ps5", "ex"], ["te1"])
+            if c == 17:
+                op("v", lambda: V.tensor_tensor_scan(T.ts[:], T.te[:], T.kk[:], 0.0, A.add, A.mult), ["te0", "te1", "kk"], ["ts"])
+        for dst, w, key in ((T.hw, 2 * C, "h"), (T.hx, C, "g")):
+            for b in range(4):
+                if t == 0:
+                    act(dst[:, w * b:w * b + C], T.xt0[:, lo + b:hi:4], ["xt"], [key + str(b)], scale=0.5)
+                else:
+                    act(dst[:, w * b:w * b + C], T.uu[:, C * b:C * b + C], ["uu%d_0" % b, "uu%d_1" % b], [key + str(b)], scale=2.0 ** -6)
+        for b in range(4):
+            k = "ps%d" % (1 + b)
+            mm(T[k][:, 0:C], T.eq[:, 128 * b:128 * b + 128], T.es[:, 128 * b:128 * b + 128], T["qp%d" % t][:], T["sp%d" % t][:], ["eq%d" % b, "qp%d" % t], [k])
+            act(T.hw[:, 2 * C * b + C:2 * C * b + 2 * C], T[k][:, 0:C], [k], ["d%d" % b], scale=0.5)
+        if t == 0:
+            for i, k in enumerate((0, hi)):
+                act(T.xt1[:, k:k + lo], T.xt0[:, k:k + lo], ["xt"], ["xpad%d" % i])
+        tt(T.pli[:], T.acc[:], T.ts[:, 15:C:16], A.subtract, ["acc%d" % c for c in range(NC)] + ["ts"], ["pli"])
+        ts(T.hh[:], T.pli[:], -1.5, 0.5, [A.add, A.mult], ["pli"], ["hh"])
+        ts(T.pq[:], T.pli[:], 0.25, None, [A.mult], ["pli"], ["pq"])
+        ts(T.plu[:], T.pli[:], -1.0, None, [A.add], ["pli"], ["plu"])
+        tt(T.pxi[:], T.hh[:], T.pq[:], A.subtract, ["hh", "pq"], ["pxi"])
+        cp(T.wo[:].indirect(T.plu[:]), T.vb[:], ["plu", "vb"], ["wo"])
+        ts(T.pxu[:], T.pxi[:], 4.0, 2.0, [A.mult, A.add], ["pxi"], ["pxu"])
+        cp(T.gb[:, 16:16 + C], T.wo[:].indirect(T.pxu[:]), ["wo", "pxu"], ["gb"])
+        turn(0, T.gb[:, 16:16 + C], ["gb", "ta1"], "ta0")
+        turn(C, T.gb[:], ["gb", "gb_pad", "tb1"], "tb0")
+        cp(T.bl[:], turned, ["ta0", "tb0"] + wlk, ["bl"])
+        tt(T.qb[:], turned, T.kb[:], A.subtract, ["ta0", "tb0", "kb", "kb_pad20"] + wlk, ["qb"])
+        tt(T.qa[:], turned, T.ka[:], A.subtract, ["ta0", "tb0", "ka", "ka_pad20"] + wlk, ["qa"])
+        tt(T.xb[:], T.bl[:, 0:NC], T.qb[:, 0:NC], A.subtract, ["bl", "qb"], ["xb"])
+        ts(T.ca[:], T.qa[:, 0:NC], -0.4, C - 0.6, [A.max, A.min], ["qa"], ["ca"])
+        tt(T.dl[:], T.bl[:, 0:NC], lw[:], A.subtract, ["bl", lk], ["dl"])
+        ts(T.cb[:], T.xb[:], 0.0, (C - 1) / 512.0, [A.max, A.min], ["xb"], ["cb"])
+        tt(T.oa[:], T.ca[:], T.qa[:, 0:NC], A.is_equal, ["ca", "qa"], ["oa"])
+        ts(T.e5[:], T.xb[:], -512.0, None, [A.mult], ["xb"], ["e5"])
+        tt(T.ob[:], T.cb[:], T.xb[:], A.is_equal, ["cb", "xb"], ["ob"])
+        tt(T.m1[:], T.oa[:], T.dl[:], A.mult, ["oa", "dl"], ["m1"])
+        tt(T.db[:], T.f1[:], T.e5[:], A.add, ["f1", "e5"], ["db"])
+        tt(T.md[:], T.m1[:], T.ob[:], A.mult, ["m1", "ob"], ["md"])
+        tt(T.mm[:], T.oa[:], T.ob[:], A.mult, ["oa", "ob"], ["mm"])
+        tt(ln[:], lw[:], T.md[:], A.add, [lk, "md"], ["lw%d" % (t + 1)])
+        tt(T.pm[:], T.mm[:], T.db[:], A.mult, ["mm", "db"], ["pm"])
+        lu, luk = T["lu%d" % t], "lu%d" % t
+        cp(lu[:], ln[:], ["lw%d" % (t + 1)], [luk])
+        send(T["la%d" % t][:], lu[:], "rl%d" % t, "ll%d" % t, [luk])
+        tt(T.pf[:], T.pm[:], T.iw[:], A.add, ["pm", "iw"], ["pf"])
+        cp(T.wb[:, C:3 * C].indirect(lu[:]), T.iof[:], [luk, "iof"], ["wb"])
+        cp(T.pu[:], T.pf[:], ["pf"], ["pu"])
+        l5, l5k = T["l5%d" % t], "l5%d" % t
+        if t + 1 < ROUNDS:
+            act(T["l5%d" % (t + 1)][:], l5[:].indirect(T.pu[:]), [l5k, "pu"], ["l5%d" % (t + 1)])
+            tt(T.vb[:], l5[:].indirect(T.pu[:]), T.iov[:], A.add, [l5k, "pu", "iov"], ["vb"])
+        else:
+            act(T.olb[:], l5[:].indirect(T.pu[:]), [l5k, "pu"], ["olb"])
+            dma("s", T.ol[:], T.olb[0:128:16, :], "dol", ["olb"], [])
+            quant(T.vq[:], T.vs[:], T.vt[:], ["vt"], ["vq"])
+        cp(T.wb[:, 0:2 * C].indirect(T["la%d" % t][:]), T.iog[:], ["la%d" % t, "iog"], ["wb"])
+        turn(0, T.wb[:, C:2 * C], ["wb"], "ta0")
+        turn(C, T.wb[:, C - 16:2 * C + 16], ["wb"], "tb0")
+        cp(T.eu[:], turned, ["ta0", "tb0"] + wlk, ["eu"])
+        for b, h, n in ((0, 0, 2), (1, 0, 2), (2, 0, 2), (3, 0, 1), (3, 1, 1)):
+            o, j, w = 2 * C * b, M * h, M * n
+            zk = ["z%d_%d" % (b, i) for i in range(h, h + n)]
+            tt(T.z[:, 4 * j + b:4 * (j + w):4], T.hw[:, o:o + 2 * C].indirect(T.eu[:, j // 16:(j + w) // 16]), T.hx[:, C * b + j:C * b + j + w], A.add,
+               ["eu", "h%d" % b, "g%d" % b, "d%d" % b], zk)
+            act(T.z32[:, C * b + j:C * b + j + w], T.z[:, 4 * j + b:4 * (j + w):4], zk, ["zz%d_%d" % (b, i) for i in range(h, h + n)], scale=32.0)
+        banks = (("ps6", "ps7", "ps1", "ps2"), ("ps3", "ps4", "ps0", "ps5"))
+        for h in range(2):
+            j = M * h
+            quant(T.zq[:, j:j + M], T.zs[:, j:j + M], T.z[:, 4 * j:4 * (j + M)], ["z%d_%d" % (b, h) for b in range(4)], ["zq%d" % h])
+            for b in range(4):
+                k = banks[h][b]
+                mm(T[k][:, 0:M], T.wq[:, 128 * b:128 * b + 128], T.wp[:, 128 * b:128 * b + 128], T.zq[:, j:j + M], T.zs[:, j:j + M], ["w", "zq%d" % h], [k])
+        for h in range(2):
+            j = M * h
+            for b in range(4):
+                k, u = banks[h][b], T.uu[:, C * b + j:C * b + j + M]
+                tt(u, T[k][:, 0:M], T.z32[:, C * b + j:C * b + j + M], A.add, [k, "zz%d_%d" % (b, h)], ["uu%d_%d" % (b, h)])
+                if b < 3:
+                    act(T.xt1[:, lo + 4 * j + b:lo + 4 * (j + M):4], u, ["uu%d_%d" % (b, h)], ["x%d_%d" % (b, h)], scale=2.0 ** -5)
+                if (b, h) == (0, 1):
+                    ts(T.xt1[:, lo + 3:lo + 4 * M:4], T.uu[:, 3 * C:3 * C + M], 2.0 ** -5, None, [A.mult], ["uu3_0"], ["x3_0"])
+
+    q3, s3 = T["qx%d" % ROUNDS], T["sx%d" % ROUNDS]
+    for h in range(2):
+        j, k = M * h, ("ps6", "ps7")[h]
+        if h:
+            ts(T.xt1[:, lo + 4 * M + 3:hi:4], T.uu[:, 3 * C + M:4 * C], 2.0 ** -5, None, [A.mult], ["uu3_1"], ["x3_1"])
+        quant(q3[:, j:j + M], s3[:, j:j + M], T.xt1[:, lo + 4 * j:lo + 4 * (j + M)], ["x%d_%d" % (b, h) for b in range(4)], ["q3_%d" % h])
+        mm(T[k][:, 0:M], T.vq[:], T.vs[:], q3[:, j:j + M], s3[:, j:j + M], ["vq", "q3_%d" % h], [k])
+    for h in range(2):
+        j, k = M * h, ("ps6", "ps7")[h]
+        cp(T.yb[:, j:j + M], T[k][:, 0:M], [k], ["yb%d" % h])
+        dma("as"[h], T.y[:, j:j + M], T.yb[:, j:j + M], "dy", ["yb%d" % h], [])
+    qk = ["q3_0", "q3_1"]
+    dma("a", T.oc[:], q3[:].bitcast(dt.uint8), "doc", qk, [])
+    for k in range(4):
+        dma("s" if k % 2 else "a", T.osc[4 * k:4 * k + 4, :], s3[32 * k:32 * k + 4, :], "doc", qk, [])
+    for t in range(ROUNDS):
+        count["rq%d" % t], count["rl%d" % t] = 2 * nmask, nmask
+    need("s", [(s, m) for s, m in count.items()])

@@ -1,12 +1,17 @@
-from concourse.mybir import dt, AluOpType, ActivationFunctionType, AxisListType
+from concourse.mybir import dt, AluOpType, ActivationFunctionType
 
 A = AluOpType
-COPY = ActivationFunctionType.Copy
+F = ActivationFunctionType
 C, ROUNDS = 320, 3
 E = C + 32
 M = C // 2
 NC = C // 16
+NS = 2
+NV = NC - 1 - NS
+BIG = 2.0 ** 96
+WHOLE = 1.5 * 2.0 ** 23
 F8 = "float8_e4m3fn_x4"
+WIDTH = (128, 128, 192, 256, 320)
 
 SCRATCH = {}
 
@@ -16,40 +21,44 @@ def _declare(names, columns, dtype, where="sbuf"):
         SCRATCH[name] = (where, [128, columns], dtype)
 
 
-_declare("xt0 xt1", 4 * E, "bfloat16")
-_declare("z z32 uu hx", 4 * C, "bfloat16")
-_declare("ut vt", 512, "bfloat16")
+_declare("xt0 xt1 z z32 uu hx", 4 * C, "bfloat16")
+_declare("ut vt gi bo", 512, "bfloat16")
 _declare("eo ee", 516, "bfloat16")
 _declare("hw", 8 * C, "bfloat16")
 _declare("fb", NC * C, "bfloat16")
-_declare("te ts kk", C, "bfloat16")
-_declare("uq uqr vq", 128, F8)
-_declare("us usr vs", 128, "uint8")
+_declare("sg", NS * C, "bfloat16")
+_declare("mk rs dlt r0 sd ca cs iob", C, "bfloat16")
+_declare("wb", 2 * C + 32, "bfloat16")
+_declare("tu tl", C + E, "bfloat16")
+for _k, _n in enumerate(WIDTH):
+    _declare("bt%d" % _k, 4 * _n, "bfloat16")
+_declare("bq", 1024, F8)
+_declare("bs", 1024, "uint8")
+_declare("uq uqr vq oq", 128, F8)
+_declare("us usr vs os_", 128, "uint8")
 _declare("wq eq", 512, F8)
 _declare("wp es", 512, "uint8")
-_declare("zq qx3 qp0 qp1 qp2", C, F8)
-_declare("zs sx3 sp0 sp1 sp2", C, "uint8")
-_declare("qx0 qx1 qx2", E, F8)
-_declare("sx0 sx1 sx2", E, "uint8")
-_declare("gb", E, "float32")
-_declare("wb", 3 * C, "float32")
-_declare("tt", C + E, "float32")
-_declare("nb ex vb wo j16 iof iog iov yb olb l50 l51 l52", C, "float32")
-_declare("sw qa qb ka kb", 32, "float32")
-_declare("acc pq pxi xb ca cb oa ob dl ls m1 md mm e5 f1 db pm pf ci iw pbf lw0 lw1 lw2 lw3", NC, "float32")
-_declare("qf q20 k1 k2 k3", 1, "float32")
-_declare("pli hh pin", NC, "int32")
-_declare("bl", 32, "int32")
+_declare("zq qx0 qx1 qx2 qx3 qp0 qp1 qp2", C, F8)
+_declare("zs sx0 sx1 sx2 sx3 sp0 sp1 sp2", C, "uint8")
+_declare("m1 exm vb wo gb gs j16 iof iov yb olb l4 l50 l51 l52", C, "float32")
+_declare("lo", 32, "float32")
+_declare("up0 up1 up2", 32, "bfloat16")
+_declare("la0 la1 la2", NC, "bfloat16")
+_declare("acc kr ci iw ef", NC, "float32")
+_declare("qf gf q20 k1 k2 k3", 1, "float32")
+_declare("pin lw1 lw2 lw3", NC, "int32")
+SMALL = {"wf": "ab ac pq pxi kb o1 dl mi o34 md bt bu mm pm pf ahi alo ka ia pbf".split(), "wi": "pli hh lb yi pg".split()}
+_declare("wf", NC * len(SMALL["wf"]), "float32")
+_declare("wi", NC * len(SMALL["wi"]), "int32")
 _declare("pb", C, "int32")
 _declare("c8", 8, "int32")
-_declare("pi qi oi si ri", 1, "int32")
-_declare("plu pxu pu exl pbl lu0 lu1 lu2 la0 la1 la2", NC, "uint16")
-_declare("eu", 32, "uint16")
+_declare("pi qi oi si ri gj", 1, "int32")
+_declare("plu pxu pu pbl lu eu", NC, "uint16")
 _declare("ul", 8, "uint16")
 _declare("wl", 2, "uint16")
 _declare("ps0 ps1 ps2 ps3 ps4 ps5 ps6 ps7", 512, "float32", "psum")
 
-SEMAPHORES = (["v", "a", "t", "gc_", "dx", "du", "dp", "dpb", "dw", "dv", "dy", "dol", "doc"]
+SEMAPHORES = (["v", "a", "t", "gc_", "dx0", "dx1", "du", "dp", "dpb", "dw", "dv", "dy", "dol", "doc"]
               + ["%s%d" % (n, t) for n in ("rq", "rl", "lq", "ll") for t in range(ROUNDS)])
 
 
@@ -97,8 +106,8 @@ def rank_program(g, core, T, topo):
             wrote[k] = tok
             read[k] = {}
 
-    def op(q, fn, reads, writes):
-        need(q, deps(q, reads, writes))
+    def op(q, fn, reads, writes, free=()):
+        need(q, [k for k in deps(q, reads, writes) if k not in free])
         fn().then_inc(T.sem[q], 1)
         count[q] = count.get(q, 0) + 1
         note((q, count[q]), reads, writes, q)
@@ -115,6 +124,7 @@ def rank_program(g, core, T, topo):
         count[lsem] = count.get(lsem, 0) + nmask
 
     V, S, P = g.vector, g.scalar, g.tensor
+    W = {n: T[b][:, NC * i:NC * i + NC] for b, names in SMALL.items() for i, n in enumerate(names)}
 
     def tt(out, a, b, o, reads, writes):
         op("v", lambda: V.tensor_tensor(out, a, b, o), reads, writes)
@@ -128,28 +138,36 @@ def rank_program(g, core, T, topo):
     def cp(out, a, reads, writes):
         op("v", lambda: V.tensor_copy(out, a), reads, writes)
 
-    def act(out, a, reads, writes, scale=1.0, accum=None):
-        op("a", lambda: S.activation(out, a, COPY, scale=scale, accum_out=accum), reads, writes)
+    def scan(out, a, b, o, reads, writes):
+        op("v", lambda: V.tensor_tensor_scan(out, a, b, 0.0, o[0], o[1]), reads, writes)
+
+    def fill(out, value, key):
+        op("v", lambda: V.memset(out, value), [], [key])
+
+    def act(out, a, reads, writes, scale=1.0, accum=None, func=F.Copy, bias=None):
+        if bias is None:
+            op("a", lambda: S.activation(out, a, func, scale=scale, accum_out=accum), reads, writes)
+        else:
+            op("a", lambda: S.activation(out, a, func, bias=bias, scale=scale, accum_out=accum), reads, writes)
 
     def quant(q, s, a, reads, writes):
         op("v", lambda: V.quantize_mx(q, s, a), reads, writes)
 
-    def mm(out, lq, ls, rq, rs, reads, writes):
-        op("t", lambda: P.matmul_mx(out, lq, ls, rq, rs, True, True), reads, writes)
+    def mm(out, lq, ls, rq, rs, reads, writes, start=True, stop=True):
+        free = () if start else [wrote[k] for k in writes]
+        op("t", lambda: P.matmul_mx(out, lq, ls, rq, rs, start, stop), reads, writes, free)
 
     for t in range(ROUNDS):
         wrote["qp%d" % t] = ("rq%d" % t, 2 * nmask)
         wrote["la%d" % t] = ("rl%d" % t, nmask)
 
-    lo, hi = 4 * 16, 4 * (16 + C)
-    dma("s", T.xt0[:, lo:hi], T.x[:], "dx", [], [])
     dma("a", T.ut[:], T.u[:], "du", [], ["ut"])
-    dma("s", T.xt0[:, 0:lo], T.x[:, 0:lo], "dx", [], [])
-    dma("s", T.xt0[:, hi:hi + lo], T.x[:, 0:lo], "dx", [], ["xt"])
+    dma("s", T.xt0[:, 0:4 * M], T.x[:, 0:4 * M], "dx0", [], ["xt_0"])
+    dma("s", T.xt0[:, 4 * M:4 * C], T.x[:, 4 * M:4 * C], "dx1", [], ["xt_1"])
     for r in range(16):
-        dma("a", T.pb[r:128:16, :], T.p[:], "dpb", [], [])
+        dma("s", T.pb[r:128:16, :], T.p[:], "dpb", [], [])
     wrote["pb"] = ("dpb", count["dpb"])
-    dma("s", T.pin[:], T.p[:], "dp", [], ["pin"])
+    dma("s", T.pin[:], T.p[:], "dp", [], ["lw0"])
     dma("s", T.wq[:].bitcast(dt.uint8), T.wc[:], "dw", [], [])
     dma("s", T.wp[:], T.ws[:], "dw", [], ["w"])
     dma("s", T.vt[:], T.v[:], "dv", [], ["vt"])
@@ -157,148 +175,199 @@ def rank_program(g, core, T, topo):
     def iota(out, pattern, base, mul, key):
         op("gc_", lambda: g.iota(out, pattern, base, mul, allow_small_or_imprecise_dtypes=True), [], [key])
 
-    op("v", lambda: V.memset(T.eo[:], 1.0), [], ["eo"])
-    for name, k, w in (("gb", 0, 16), ("gb", C + 16, 16), ("wb", C - 16, 16), ("wb", 2 * C, 16), ("ka", 20, 12), ("kb", 20, 12)):
-        op("v", lambda: V.memset(T[name][:, k:k + w], 0.0), [], ["%s_pad%d" % (name, k)])
-    wrote["gb_pad"], wrote["wb"] = wrote["gb_pad%d" % (C + 16)], wrote["wb_pad%d" % (2 * C)]
+    fill(T.eo[:], 1.0, "eo")
+    for k, n in enumerate(WIDTH):
+        fill(T["bt%d" % k][:, 4 * 16 * (4 * k + 1):4 * n], 0.0, "bz%d" % k)
+    fill(T.wb[:, 16:16 + C], float(C), "wb_a")
+    fill(T.wb[:, 0:16], 0.0, "wb_b")
+    fill(T.wb[:, 16 + C:32 + 2 * C], 0.0, "wb")
+    fill(T.acc[:, 0:1], 0.0, "acc0")
     iota(T.c8[:], [[16, 8]], 0, 0, "c8")
     iota(T.pi[:], [[1, 1]], 0, 1, "pi")
     iota(T.ci[:], [[1, NC]], 0, 0, "ci")
     iota(T.j16[:], [[0, NC], [1, 16]], 0, 0, "j16")
-    op("gc_", lambda: g.affine_select(T.ee[:], T.eo[:], [[1, 516]], A.is_equal, 0.0, -3, -4), ["eo"], ["ee"])
-    iota(T.iof[:], [[1, C]], 0, 0, "iof")
+    iota(T.gi[:], [[1, 8], [0, 64]], 0, 0, "gi")
+    iota(T.iof[:], [[1, C]], -M, 0, "iof")
     cp(T.ul[:], T.c8[:], ["c8"], ["ul"])
     ts(T.qi[:], T.pi[:], 15, None, [A.bitwise_and], ["pi"], ["qi"])
     ts(T.oi[:], T.pi[:], 16, 4, [A.bitwise_and, A.arith_shift_right], ["pi"], ["oi"])
-    cp(T.exl[:], T.ci[:], ["ci"], ["exl"])
+    ts(T.gj[:], T.pi[:], 4, None, [A.arith_shift_right], ["pi"], ["gj"])
     cp(T.qf[:], T.qi[:], ["qi"], ["qf"])
     tt(T.si[:], T.qi[:], T.oi[:], A.add, ["qi", "oi"], ["si"])
     ts(T.k2[:], T.qi[:], 16.0, None, [A.mult], ["qi"], ["k2"])
+    cp(T.gf[:], T.gj[:], ["gj"], ["gf"])
     ts(T.q20[:], T.qf[:], 20.0, None, [A.mult], ["qf"], ["q20"])
     ts(T.ri[:], T.si[:], 1, None, [A.bitwise_and], ["si"], ["ri"])
     ts(T.iw[:], T.ci[:], 16.0, T.qf[:, 0:1], [A.mult, A.add], ["ci", "qf"], ["iw"])
+    ts(W["pbf"], T.ci[:], T.q20[:, 0:1], None, [A.add], ["ci", "q20"], ["pbf"])
     ts(T.k1[:], T.ri[:], float(C + 16), None, [A.mult], ["ri"], ["k1"])
-    ts(T.pbf[:], T.ci[:], T.q20[:, 0:1], None, [A.add], ["ci", "q20"], ["pbf"])
+    ts(T.dlt[:], T.j16[:], T.qf[:, 0:1], None, [A.is_equal], ["j16", "qf"], ["dlt"])
+    ts(T.r0[:], T.j16[:], 0.0, None, [A.is_gt], ["j16"], ["r0"])
     tt(T.k3[:], T.k1[:], T.k2[:], A.add, ["k1", "k2"], ["k3"])
-    cp(T.ka[:, 0:NC], T.iw[:], ["iw"], ["ka"])
-    cp(T.pbl[:], T.pbf[:], ["pbf"], ["pbl"])
-    cp(T.wl[:, 0:1], T.k3[:], ["k3"], ["wl0"])
-    ts(T.wl[:, 1:2], T.k3[:], 256.0, float(C + E - 1), [A.add, A.min], ["k3"], ["wl1"])
-    ts(T.kk[:], T.j16[:], T.qf[:, 0:1], None, [A.is_gt], ["j16", "qf"], ["kk"])
+    cp(T.pbl[:], W["pbf"], ["pbf"], ["pbl"])
+    ts(T.mk[:], T.dlt[:], -0.5, 2 * BIG, [A.add, A.mult], ["dlt"], ["mk"])
+    ts(T.rs[:], T.r0[:], -0.5, 2 * BIG, [A.add, A.mult], ["r0"], ["rs"])
 
     quant(T.uq[:], T.us[:], T.ut[:], ["ut"], ["uq"])
+    cp(T.wl[:, 0:1], T.k3[:], ["k3"], ["wl0"])
     op("v", lambda: V.tensor_copy(T.uqr[:, 0:128].bitcast(dt.uint32), T.uq[:, 0:128].bitcast(dt.uint32).indirect(T.ul[:, 0:8])), ["uq", "ul"], ["uqr"])
     op("v", lambda: V.tensor_copy(T.usr[:, 0:128], T.us[:, 0:128].indirect(T.ul[:, 0:8])), ["uq", "ul"], ["usr"])
-    for b in range(4):
-        quant(T.eq[:, 128 * b:128 * b + 128], T.es[:, 128 * b:128 * b + 128], T.ee[:, 3 - b:515 - b], ["ee"], ["eq%d" % b])
 
-    def turn(at, in_, keys, key):
-        w = in_.shape[1]
-        op("v", lambda: V.transpose(T.tt[:, at:at + w], in_), keys, [key])
+    def later_constants():
+        ts(T.wl[:, 1:2], T.k3[:], 256.0, float(C + E - 1), [A.add, A.min], ["k3"], ["wl1"])
+        ts(T.bo[:], T.gi[:], T.gf[:, 0:1], None, [A.is_equal], ["gi", "gf"], ["bo"])
+        ts(T.kr[:, 0:NV + 1], T.ci[:, 0:NV + 1], 0.0, 8.0 * NV + 15, [A.mult, A.add], ["ci"], ["kr_a"])
+        ts(T.kr[:, NV + 1:NC], T.ci[:, NV + 1:NC], 16.0, 15.0, [A.mult, A.add], ["ci"], ["kr_b"])
+        quant(T.oq[:], T.os_[:], T.bo[:], ["bo"], ["oq"])
+        ts(T.kr[:], T.kr[:], T.qf[:, 0:1], None, [A.subtract], ["kr_a", "kr_b", "qf"], ["kr"])
 
-    turned = T.tt[:].indirect(T.wl[:])
+    def exchange_constants():
+        ts(W["ahi"], T.iw[:], C - 0.6, None, [A.add], ["iw"], ["ahi"])
+        ts(W["alo"], T.iw[:], -0.5, None, [A.add], ["iw"], ["alo"])
+        ts(W["ka"], T.iw[:], 0.5 - M, -1.0 / C, [A.add, A.mult], ["iw"], ["ka"])
+        ts(W["ia"], T.iw[:], 1.0 / C, None, [A.mult], ["iw"], ["ia"])
+
+    def turn(name, at):
+        op("v", lambda: V.transpose(T[name][:, 0:C], T.wb[:, at + 16:at + 16 + C]), ["wb"], [name + "a"])
+        op("v", lambda: V.transpose(T[name][:, C:C + E], T.wb[:, at:at + E]), ["wb", "wb_a", "wb_b"], [name + "b"])
+
     wlk = ["wl0", "wl1"]
+    last = slice(15, C, 16)
 
     for t in range(ROUNDS):
         xt = T.xt0 if t == 0 else T.xt1
         qx, sx, qk = T["qx%d" % t], T["sx%d" % t], ["qx%d_0" % t, "qx%d_1" % t]
-        if t == 0:
-            quant(qx[:, 0:16 + M], sx[:, 0:16 + M], xt[:, 0:lo + 4 * M], ["xt"], qk[:1])
-            quant(qx[:, 16 + M:E], sx[:, 16 + M:E], xt[:, lo + 4 * M:4 * E], ["xt"], qk[1:])
-        else:
-            quant(qx[:, 0:16 + M], sx[:, 0:16 + M], xt[:, 0:lo + 4 * M], ["x%d_0" % b for b in range(4)] + ["xpad0"], qk[:1])
-            ts(xt[:, lo + 4 * M + 3:hi:4], T.uu[:, 3 * C + M:4 * C], 2.0 ** -5, None, [A.mult], ["uu3_1"], ["x3_1"])
-            quant(qx[:, 16 + M:E], sx[:, 16 + M:E], xt[:, lo + 4 * M:4 * E], ["x%d_1" % b for b in range(4)] + ["xpad1"], qk[1:])
+        lw, ln, lk = T["pin" if t == 0 else "lw%d" % t], T["lw%d" % (t + 1)], "lw%d" % t
+        for h in range(2):
+            j = M * h
+            if t and h:
+                ts(xt[:, 4 * M + 3:4 * C:4], T.uu[:, 3 * C + M:4 * C], 2.0 ** -5, None, [A.mult], ["uu3_1"], ["x3_1"])
+            quant(qx[:, j:j + M], sx[:, j:j + M], xt[:, 4 * j:4 * (j + M)], ["x%d_%d" % (b, h) for b in range(4)] if t else ["xt_%d" % h], [qk[h]])
         uk = ["uqr", "usr"]
-        mm(T.ps6[:, 0:16 + M], T.uqr[:], T.usr[:], qx[:, 0:16 + M], sx[:, 0:16 + M], uk + qk[:1], ["ps6"])
-        mm(T.ps0[:, 0:M], T.uqr[:], T.usr[:], qx[:, 16:16 + M], sx[:, 16:16 + M], uk + qk[:1], ["ps0"])
-        mm(T.ps7[:, 0:32 + M], T.uqr[:], T.usr[:], qx[:, M:E], sx[:, M:E], uk + qk, ["ps7"])
-        mm(T.ps5[:, 0:M], T.uqr[:], T.usr[:], qx[:, 16 + M:16 + C], sx[:, 16 + M:16 + C], uk + qk[1:], ["ps5"])
-        send(T["qp%d" % t][:].bitcast(dt.uint8), qx[:, 16:16 + C].bitcast(dt.uint8), "rq%d" % t, "lq%d" % t, qk)
-        send(T["sp%d" % t][:], sx[:, 16:16 + C], "rq%d" % t, "lq%d" % t, qk)
-        act(T.nb[:, 0:M], T.ps0[:, 0:M], ["ps0"], ["nb0"])
-        act(T.nb[:, M:C], T.ps5[:, 0:M], ["ps5"], ["nb1"])
+        mm(T.ps6[:, 0:M], T.uqr[:], T.usr[:], qx[:, 0:M], sx[:, 0:M], uk + qk[:1], ["ps6"])
+        mm(T.ps7[:, 0:C], T.uqr[:], T.usr[:], qx[:], sx[:], uk + qk, ["ps7"])
+        mm(T.ps1[:, 0:C], T.uqr[:], T.usr[:], qx[:], sx[:], uk + qk, ["ps1"])
+        send(T["qp%d" % t][:].bitcast(dt.uint8), qx[:].bitcast(dt.uint8), "rq%d" % t, "lq%d" % t, qk)
+        send(T["sp%d" % t][:], sx[:], "rq%d" % t, "lq%d" % t, qk)
         if t == 0:
-            iota(T.iog[:], [[1, C]], C, 0, "iog")
-            cp(T.l50[:], T.pb[:].indirect(T.pbl[:]), ["pb", "pbl"], ["l50"])
-        turn(0, T.ps6[:, 16:16 + M], ["ps6"], "ta0")
-        turn(C, T.ps6[:, 0:M], ["ps6"], "tb0")
-        turn(M, T.ps7[:, 16:16 + M], ["ps7"], "ta1")
-        turn(C + M, T.ps7[:, 0:32 + M], ["ps7"], "tb1")
-        tk = ["ta0", "tb0", "ta1", "tb1"]
-        cp(T.sw[:], turned, tk + wlk, ["sw"])
-        sk = ["nb0", "nb1", "sw"]
-        lw, ln, lk = T["lw%d" % t], T["lw%d" % (t + 1)], "lw%d" % t
-        for c in range(NC):
-            f, e, sc = C * c, 16 * c + 16, T.sw[:, c:c + 1]
-            fk = ["fl%d" % c, "fh%d" % c]
-            ts(T.fb[:, f:f + e], T.nb[:, 0:e], sc, None, [A.is_ge], sk, fk[:1])
-            if e < C:
-                ts(T.fb[:, f + e:f + C], T.nb[:, e:C], sc, None, [A.is_gt], sk, fk[1:])
-            if c == NC - 1:
-                op("v", lambda: V.tensor_reduce(T.acc[:, c:c + 1], T.fb[:, f:f + C], AxisListType.X, A.add), fk, ["acc%d" % c])
-            else:
-                act(T.fb[:, f:f + C], T.fb[:, f:f + C], fk, fk + ["acc%d" % c], accum=T.acc[:, c:c + 1])
-            if c == 4:
-                act(T.ex[:], T.sw[:].indirect(T.exl[:]), ["sw", "exl"], ["ex"])
-            if c == 8 and t == 0:
-                cp(T.lw0[:], T.pin[:], ["pin"], ["lw0"])
-                ts(T.iov[:], T.iof[:], float(-M), 2.0 ** -9, [A.add, A.mult], ["iof"], ["iov"])
-            if c == 10 and t == 0:
-                tt(T.vb[:], T.l50[:], T.iov[:], A.add, ["l50", "iov"], ["vb"])
-            if c == 15:
-                ts(T.kb[:, 0:NC], lw[:], float(-M), 2.0 ** -9, [A.add, A.mult], [lk], ["kb"])
-                tt(T.f1[:], lw[:], T.iw[:], A.subtract, [lk, "iw"], ["f1"])
-            if c == 16:
-                tt(T.te[:, 0:M], T.ps0[:, 0:M], T.ex[:, 0:M], A.is_equal, ["ps0", "ex"], ["te0"])
-                tt(T.te[:, M:C], T.ps5[:, 0:M], T.ex[:, M:C], A.is_equal, ["ps5", "ex"], ["te1"])
-            if c == 17:
-                op("v", lambda: V.tensor_tensor_scan(T.ts[:], T.te[:], T.kk[:], 0.0, A.add, A.mult), ["te0", "te1", "kk"], ["ts"])
+            op("gc_", lambda: g.affine_select(T.ee[:], T.eo[:], [[1, 516]], A.is_equal, 0.0, -3, -4), ["eo"], ["ee"])
+
+        def slot(c):
+            k = (c - 1) // 4
+            return T["bt%d" % k][:, (c - 1) % 4:4 * 16 * c:4], "b%d" % c
+
+        def own(c):
+            return T.exm[:, 16 * c + 15:16 * c + 16], "exm%d" % (16 * c // M)
+
+        def compare(c, bank):
+            (o, k), (s, sk) = slot(c), own(c)
+            ts(o, T[bank][:, 0:16 * c], s, -0.5, [A.is_lt, A.add], [bank, sk], [k])
+
+        def rowsum(c):
+            o, k = slot(c)
+            act(T.fb[:, C * c:C * c + 16 * c], o, [k], ["acc%d" % c], accum=T.acc[:, c:c + 1])
+
+        def sign(c):
+            s, sk = own(c)
+            act(T.sg[:, C * (c - NV - 1):C * (c - NV - 1) + 16 * c], T.ps1[:, 0:16 * c], ["ps1", sk], ["sg%d" % c], scale=-1.0, bias=s, func=F.Sign)
+
+        def relu(c):
+            o, k = slot(c)
+            act(o, T.sg[:, C * (c - NV - 1):C * (c - NV - 1) + 16 * c], ["sg%d" % c], [k, "acc%d" % c], func=F.Relu, accum=T.acc[:, c:c + 1])
+
+        def pack(k):
+            at, n = sum(WIDTH[:k]), WIDTH[k]
+            quant(T.bq[:, at:at + n], T.bs[:, at:at + n], T["bt%d" % k][:], ["b%d" % c for c in range(4 * k + 1, 4 * k + 5)] + ["bz%d" % k], ["bq%d" % k])
+            mm(T.ps2[:, 0:n], T.oq[:], T.os_[:], T.bq[:, at:at + n], T.bs[:, at:at + n], ["oq", "bq%d" % k], ["ps2"], start=k == 4, stop=k == 0)
+
+        def both(cs, bank):
+            for c in cs:
+                compare(c, bank)
+                rowsum(c)
+
+        tt(T.m1[:, 0:M], T.ps6[:, 0:M], T.mk[:, 0:M], A.min, ["ps6", "mk"], ["m1_0"])
+        if t == 0:
+            later_constants()
+        scan(T.exm[:, 0:M], T.rs[:, 0:M], T.m1[:, 0:M], [A.min, A.max], ["rs", "m1_0"], ["exm0"])
+        tt(T.m1[:, M:C], T.ps7[:, M:C], T.mk[:, 0:M], A.min, ["ps7", "mk"], ["m1_1"])
+        both([8], "ps6")
+        scan(T.exm[:, M:C], T.rs[:, 0:M], T.m1[:, M:C], [A.min, A.max], ["rs", "m1_1"], ["exm1"])
+        compare(7, "ps6")
+        for c in range(NC - 1, NV, -1):
+            sign(c)
+        for c in range(NC - 1, NV, -1):
+            relu(c)
+        rowsum(7)
+        tt(T.bt4[:, 3:4 * C:4], T.ps7[:, 0:C], T.exm[:], A.is_le, ["ps7", "exm0", "exm1", "bz4"], ["b20"])
+        both(range(NV, 12, -1), "ps7")
+        pack(4)
+        pack(3)
+        both([12, 11, 10, 9, 6, 5], "ps7")
+        pack(2)
+        both([4, 3, 2, 1], "ps7")
+        pack(1)
+        pack(0)
+        scan(T.sd[:], T.r0[:], T.bt4[:, 3:4 * C:4], [A.mult, A.add], ["r0", "b20"], ["sd"])
+        ts(W["kb"], lw[:], 1.0 - C, 1.0 / C, [A.add, A.mult], [lk], ["kb"])
+        if t == 0:
+            ts(T.iov[:], T.iof[:], 0.5, 1.0 / C, [A.add, A.mult], ["iof"], ["iov"])
+            cp(T.iob[:], T.iof[:], ["iof"], ["iob"])
+        tt(W["ab"], T.kr[:], T.sd[:, last], A.subtract, ["kr", "sd"], ["ab"])
+        tt(T.ca[:], T.ps2[:, 0:C], T.dlt[:], A.mult, ["ps2", "dlt"], ["ca"])
+        tt(W["ac"], W["ab"], T.acc[:], A.subtract, ["ab"] + ["acc%d" % c for c in range(NC)], ["ac"])
+        scan(T.cs[:], T.r0[:], T.ca[:], [A.mult, A.add], ["r0", "ca"], ["cs"])
+        if t == 0:
+            tt(T.vb[:], T.pb[:].indirect(T.pbl[:]), T.iov[:], A.add, ["pb", "pbl", "iov"], ["vb"])
+            act(T.l4[:], T.vb[:], ["vb"], ["l4"], func=F.Identity, bias=WHOLE)
         for dst, w, key in ((T.hw, 2 * C, "h"), (T.hx, C, "g")):
             for b in range(4):
                 if t == 0:
-                    act(dst[:, w * b:w * b + C], T.xt0[:, lo + b:hi:4], ["xt"], [key + str(b)], scale=0.5)
+                    act(dst[:, w * b:w * b + C], T.xt0[:, b:4 * C:4], ["xt_0", "xt_1"], [key + str(b)], scale=0.5)
                 else:
                     act(dst[:, w * b:w * b + C], T.uu[:, C * b:C * b + C], ["uu%d_0" % b, "uu%d_1" % b], [key + str(b)], scale=2.0 ** -6)
+        if t == 0:
+            act(T.l50[:], T.l4[:], ["l4"], ["l50"], func=F.Identity, bias=-WHOLE)
+        tt(W["pli"], W["ac"], T.cs[:, last], A.add, ["ac", "cs"], ["pli"])
+        cp(T.plu[:], W["pli"], ["pli"], ["plu"])
+        ts(W["hh"], W["pli"], -0.5, 0.5, [A.add, A.mult], ["pli"], ["hh"])
+        ts(W["pq"], W["pli"], 0.25, None, [A.mult], ["pli"], ["pq"])
+        cp(T.wo[:].indirect(T.plu[:]), T.vb[:], ["plu", "vb"], ["wo"])
+        tt(W["pxi"], W["hh"], W["pq"], A.subtract, ["hh", "pq"], ["pxi"])
+        if t == 0:
+            exchange_constants()
+        ts(T.pxu[:], W["pxi"], 4.0, 1.0, [A.mult, A.add], ["pxi"], ["pxu"])
+        if t == 0:
+            for b in range(4):
+                quant(T.eq[:, 128 * b:128 * b + 128], T.es[:, 128 * b:128 * b + 128], T.ee[:, 3 - b:515 - b], ["ee"], ["eq%d" % b])
         for b in range(4):
-            k = "ps%d" % (1 + b)
+            k = ("ps3", "ps4", "ps0", "ps5")[b]
             mm(T[k][:, 0:C], T.eq[:, 128 * b:128 * b + 128], T.es[:, 128 * b:128 * b + 128], T["qp%d" % t][:], T["sp%d" % t][:], ["eq%d" % b, "qp%d" % t], [k])
             act(T.hw[:, 2 * C * b + C:2 * C * b + 2 * C], T[k][:, 0:C], [k], ["d%d" % b], scale=0.5)
-        if t == 0:
-            for i, k in enumerate((0, hi)):
-                act(T.xt1[:, k:k + lo], T.xt0[:, k:k + lo], ["xt"], ["xpad%d" % i])
-        tt(T.pli[:], T.acc[:], T.ts[:, 15:C:16], A.subtract, ["acc%d" % c for c in range(NC)] + ["ts"], ["pli"])
-        ts(T.hh[:], T.pli[:], -1.5, 0.5, [A.add, A.mult], ["pli"], ["hh"])
-        ts(T.pq[:], T.pli[:], 0.25, None, [A.mult], ["pli"], ["pq"])
-        ts(T.plu[:], T.pli[:], -1.0, None, [A.add], ["pli"], ["plu"])
-        tt(T.pxi[:], T.hh[:], T.pq[:], A.subtract, ["hh", "pq"], ["pxi"])
-        cp(T.wo[:].indirect(T.plu[:]), T.vb[:], ["plu", "vb"], ["wo"])
-        ts(T.pxu[:], T.pxi[:], 4.0, 2.0, [A.mult, A.add], ["pxi"], ["pxu"])
-        cp(T.gb[:, 16:16 + C], T.wo[:].indirect(T.pxu[:]), ["wo", "pxu"], ["gb"])
-        turn(0, T.gb[:, 16:16 + C], ["gb", "ta1"], "ta0")
-        turn(C, T.gb[:], ["gb", "gb_pad", "tb1"], "tb0")
-        cp(T.bl[:], turned, ["ta0", "tb0"] + wlk, ["bl"])
-        tt(T.qb[:], turned, T.kb[:], A.subtract, ["ta0", "tb0", "kb", "kb_pad20"] + wlk, ["qb"])
-        tt(T.qa[:], turned, T.ka[:], A.subtract, ["ta0", "tb0", "ka", "ka_pad20"] + wlk, ["qa"])
-        tt(T.xb[:], T.bl[:, 0:NC], T.qb[:, 0:NC], A.subtract, ["bl", "qb"], ["xb"])
-        ts(T.ca[:], T.qa[:, 0:NC], -0.4, C - 0.6, [A.max, A.min], ["qa"], ["ca"])
-        tt(T.dl[:], T.bl[:, 0:NC], lw[:], A.subtract, ["bl", lk], ["dl"])
-        ts(T.cb[:], T.xb[:], 0.0, (C - 1) / 512.0, [A.max, A.min], ["xb"], ["cb"])
-        tt(T.oa[:], T.ca[:], T.qa[:, 0:NC], A.is_equal, ["ca", "qa"], ["oa"])
-        ts(T.e5[:], T.xb[:], -512.0, None, [A.mult], ["xb"], ["e5"])
-        tt(T.ob[:], T.cb[:], T.xb[:], A.is_equal, ["cb", "xb"], ["ob"])
-        tt(T.m1[:], T.oa[:], T.dl[:], A.mult, ["oa", "dl"], ["m1"])
-        tt(T.db[:], T.f1[:], T.e5[:], A.add, ["f1", "e5"], ["db"])
-        tt(T.md[:], T.m1[:], T.ob[:], A.mult, ["m1", "ob"], ["md"])
-        tt(T.mm[:], T.oa[:], T.ob[:], A.mult, ["oa", "ob"], ["mm"])
-        tt(ln[:], lw[:], T.md[:], A.add, [lk, "md"], ["lw%d" % (t + 1)])
-        tt(T.pm[:], T.mm[:], T.db[:], A.mult, ["mm", "db"], ["pm"])
-        lu, luk = T["lu%d" % t], "lu%d" % t
-        cp(lu[:], ln[:], ["lw%d" % (t + 1)], [luk])
-        send(T["la%d" % t][:], lu[:], "rl%d" % t, "ll%d" % t, [luk])
-        tt(T.pf[:], T.pm[:], T.iw[:], A.add, ["pm", "iw"], ["pf"])
-        cp(T.wb[:, C:3 * C].indirect(lu[:]), T.iof[:], [luk, "iof"], ["wb"])
-        cp(T.pu[:], T.pf[:], ["pf"], ["pu"])
+        tt(T.gb[:], T.wo[:].indirect(T.pxu[:]), T.dlt[:], A.mult, ["wo", "pxu", "dlt"], ["gb"])
+        scan(T.gs[:], T.r0[:], T.gb[:], [A.mult, A.add], ["r0", "gb"], ["gs"])
+        v = T.gs[:, last]
+        tt(W["lb"], v, W["ahi"], A.min, ["gs", "ahi"], ["lb"])
+        tt(W["yi"], v, W["kb"], A.subtract, ["gs", "kb"], ["yi"])
+        tt(W["o1"], v, W["alo"], A.is_ge, ["gs", "alo"], ["o1"])
+        tt(W["dl"], v, lw[:], A.subtract, ["gs", lk], ["dl"])
+        tt(W["o34"], W["yi"], W["lb"], A.is_equal, ["yi", "lb"], ["o34"])
+        tt(W["mi"], W["o1"], W["dl"], A.mult, ["o1", "dl"], ["mi"])
+        tt(W["bt"], v, W["lb"], A.subtract, ["gs", "lb"], ["bt"])
+        tt(W["md"], W["mi"], W["o34"], A.mult, ["mi", "o34"], ["md"])
+        tt(W["mm"], W["o1"], W["o34"], A.mult, ["o1", "o34"], ["mm"])
+        tt(ln[:], lw[:], W["md"], A.add, [lk, "md"], ["lw%d" % (t + 1)])
+        tt(W["bu"], W["bt"], W["ka"], A.add, ["bt", "ka"], ["bu"])
+        cp(T.lu[:], ln[:], ["lw%d" % (t + 1)], ["lu"])
+        tt(W["pm"], W["mm"], W["bu"], A.mult, ["mm", "bu"], ["pm"])
+        cp(T.wb[:, 16:16 + 2 * C].indirect(T.lu[:]), T.iob[:], ["lu", "iob", "wb_a"], ["wb"])
+        tt(W["pf"], W["pm"], W["ia"], A.add, ["pm", "ia"], ["pf"])
+        turn("tu", C)
+        ts(W["pg"], W["pf"], float(C), None, [A.mult], ["pf"], ["pg"])
+        up = "up%d" % t
+        cp(T[up][:], T.tu[:].indirect(T.wl[:]), ["tua", "tub"] + wlk, [up])
+        send(T["la%d" % t][:], T[up][:, 0:NC], "rl%d" % t, "ll%d" % t, [up])
+        cp(T.pu[:], W["pg"], ["pg"], ["pu"])
+        turn("tl", 0)
         l5, l5k = T["l5%d" % t], "l5%d" % t
         if t + 1 < ROUNDS:
             act(T["l5%d" % (t + 1)][:], l5[:].indirect(T.pu[:]), [l5k, "pu"], ["l5%d" % (t + 1)])
@@ -307,10 +376,9 @@ def rank_program(g, core, T, topo):
             act(T.olb[:], l5[:].indirect(T.pu[:]), [l5k, "pu"], ["olb"])
             dma("s", T.ol[:], T.olb[0:128:16, :], "dol", ["olb"], [])
             quant(T.vq[:], T.vs[:], T.vt[:], ["vt"], ["vq"])
-        cp(T.wb[:, 0:2 * C].indirect(T["la%d" % t][:]), T.iog[:], ["la%d" % t, "iog"], ["wb"])
-        turn(0, T.wb[:, C:2 * C], ["wb"], "ta0")
-        turn(C, T.wb[:, C - 16:2 * C + 16], ["wb"], "tb0")
-        cp(T.eu[:], turned, ["ta0", "tb0"] + wlk, ["eu"])
+        ts(T.lo[:], T.tl[:].indirect(T.wl[:]), float(M), None, [A.add], ["tla", "tlb"] + wlk, ["lo"])
+        tt(T.ef[:], T.lo[:, 0:NC], T["la%d" % t][:], A.add, ["lo", "la%d" % t], ["ef"])
+        cp(T.eu[:], T.ef[:], ["ef"], ["eu"])
         for b, h, n in ((0, 0, 2), (1, 0, 2), (2, 0, 2), (3, 0, 1), (3, 1, 1)):
             o, j, w = 2 * C * b, M * h, M * n
             zk = ["z%d_%d" % (b, i) for i in range(h, h + n)]
@@ -330,16 +398,16 @@ def rank_program(g, core, T, topo):
                 k, u = banks[h][b], T.uu[:, C * b + j:C * b + j + M]
                 tt(u, T[k][:, 0:M], T.z32[:, C * b + j:C * b + j + M], A.add, [k, "zz%d_%d" % (b, h)], ["uu%d_%d" % (b, h)])
                 if b < 3:
-                    act(T.xt1[:, lo + 4 * j + b:lo + 4 * (j + M):4], u, ["uu%d_%d" % (b, h)], ["x%d_%d" % (b, h)], scale=2.0 ** -5)
+                    act(T.xt1[:, 4 * j + b:4 * (j + M):4], u, ["uu%d_%d" % (b, h)], ["x%d_%d" % (b, h)], scale=2.0 ** -5)
                 if (b, h) == (0, 1):
-                    ts(T.xt1[:, lo + 3:lo + 4 * M:4], T.uu[:, 3 * C:3 * C + M], 2.0 ** -5, None, [A.mult], ["uu3_0"], ["x3_0"])
+                    ts(T.xt1[:, 3:4 * M:4], T.uu[:, 3 * C:3 * C + M], 2.0 ** -5, None, [A.mult], ["uu3_0"], ["x3_0"])
 
     q3, s3 = T["qx%d" % ROUNDS], T["sx%d" % ROUNDS]
     for h in range(2):
         j, k = M * h, ("ps6", "ps7")[h]
         if h:
-            ts(T.xt1[:, lo + 4 * M + 3:hi:4], T.uu[:, 3 * C + M:4 * C], 2.0 ** -5, None, [A.mult], ["uu3_1"], ["x3_1"])
-        quant(q3[:, j:j + M], s3[:, j:j + M], T.xt1[:, lo + 4 * j:lo + 4 * (j + M)], ["x%d_%d" % (b, h) for b in range(4)], ["q3_%d" % h])
+            ts(T.xt1[:, 4 * M + 3:4 * C:4], T.uu[:, 3 * C + M:4 * C], 2.0 ** -5, None, [A.mult], ["uu3_1"], ["x3_1"])
+        quant(q3[:, j:j + M], s3[:, j:j + M], T.xt1[:, 4 * j:4 * (j + M)], ["x%d_%d" % (b, h) for b in range(4)], ["q3_%d" % h])
         mm(T[k][:, 0:M], T.vq[:], T.vs[:], q3[:, j:j + M], s3[:, j:j + M], ["vq", "q3_%d" % h], [k])
     for h in range(2):
         j, k = M * h, ("ps6", "ps7")[h]

@@ -6,7 +6,7 @@ C, ROUNDS = 320, 3
 E = C + 32
 M = C // 2
 NC = C // 16
-NS = 2
+NS = 3
 NV = NC - 1 - NS
 BIG = 2.0 ** 96
 WHOLE = 1.5 * 2.0 ** 23
@@ -27,7 +27,8 @@ _declare("eo ee", 516, "bfloat16")
 _declare("hw", 8 * C, "bfloat16")
 _declare("fb", NC * C, "bfloat16")
 _declare("sg", NS * C, "bfloat16")
-_declare("mk rs dlt r0 sd ca cs iob", C, "bfloat16")
+_declare("r0 sd ca cs iob", C, "bfloat16")
+_declare("j16 aa dlt mk rs", M, "bfloat16")
 _declare("wb", 2 * C + 32, "bfloat16")
 _declare("tu tl", C + E, "bfloat16")
 for _k, _n in enumerate(WIDTH):
@@ -40,19 +41,20 @@ _declare("wq eq", 512, F8)
 _declare("wp es", 512, "uint8")
 _declare("zq qx0 qx1 qx2 qx3 qp0 qp1 qp2", C, F8)
 _declare("zs sx0 sx1 sx2 sx3 sp0 sp1 sp2", C, "uint8")
-_declare("m1 exm vb wo gb gs j16 iof iov yb olb l4 l50 l51 l52", C, "float32")
+_declare("m1 exm vb wo gb gs iof iov yb olb l4 l50 l51 l52", C, "float32")
 _declare("lo", 32, "float32")
 _declare("up0 up1 up2", 32, "bfloat16")
 _declare("la0 la1 la2", NC, "bfloat16")
 _declare("acc kr ci iw ef", NC, "float32")
-_declare("qf gf q20 k1 k2 k3", 1, "float32")
+_declare("qf gf", 1, "float32")
+_declare("kk", 10, "float32")
 _declare("pin lw1 lw2 lw3", NC, "int32")
 SMALL = {"wf": "ab ac pq pxi kb o1 dl mi o34 md bt bu mm pm pf ahi alo ka ia pbf".split(), "wi": "pli hh lb yi pg".split()}
 _declare("wf", NC * len(SMALL["wf"]), "float32")
 _declare("wi", NC * len(SMALL["wi"]), "int32")
 _declare("pb", C, "int32")
 _declare("c8", 8, "int32")
-_declare("pi qi oi si ri gj", 1, "int32")
+_declare("pi qi gj", 1, "int32")
 _declare("plu pxu pu pbl lu eu", NC, "uint16")
 _declare("ul", 8, "uint16")
 _declare("wl", 2, "uint16")
@@ -175,57 +177,90 @@ def rank_program(g, core, T, topo):
     def iota(out, pattern, base, mul, key):
         op("gc_", lambda: g.iota(out, pattern, base, mul, allow_small_or_imprecise_dtypes=True), [], [key])
 
+    def scores(t, h, product=True):
+        xt = T.xt0 if t == 0 else T.xt1
+        qx, sx, qk = T["qx%d" % t], T["sx%d" % t], ["qx%d_0" % t, "qx%d_1" % t]
+        j, uk = M * h, ["uqr", "usr"]
+        quant(qx[:, j:j + M], sx[:, j:j + M], xt[:, 4 * j:4 * (j + M)], ["x%d_%d" % (b, h) for b in range(4)] if t else ["xt_%d" % h], [qk[h]])
+        if t == ROUNDS:
+            k = ("ps6", "ps7")[h]
+            mm(T[k][:, 0:M], T.vq[:], T.vs[:], qx[:, j:j + M], sx[:, j:j + M], ["vq", qk[h]], [k])
+            dma("s", T.oc[:, 4 * j:4 * (j + M)], qx[:, j:j + M].bitcast(dt.uint8), "doc", [qk[h]], [])
+        elif h:
+            mm(T.ps7[:, 0:C], T.uqr[:], T.usr[:], qx[:], sx[:], uk + qk, ["ps7"])
+            mm(T.ps1[:, 0:C], T.uqr[:], T.usr[:], qx[:], sx[:], uk + qk, ["ps1"])
+            send(T["qp%d" % t][:].bitcast(dt.uint8), qx[:].bitcast(dt.uint8), "rq%d" % t, "lq%d" % t, qk)
+            send(T["sp%d" % t][:], sx[:], "rq%d" % t, "lq%d" % t, qk)
+        elif product:
+            mm(T.ps6[:, 0:M], T.uqr[:], T.usr[:], qx[:, 0:M], sx[:, 0:M], uk + qk[:1], ["ps6"])
+
     fill(T.eo[:], 1.0, "eo")
+    iota(T.pi[:], [[1, 1]], 0, 1, "pi")
+    iota(T.c8[:], [[16, 8]], 0, 0, "c8")
+    iota(T.j16[:], [[0, M // 16], [1, 16]], 0, 0, "j16")
+    iota(T.ci[:], [[1, NC]], 0, 0, "ci")
+    op("gc_", lambda: g.affine_select(T.gi[:], T.eo[:, 0:512], [[-16, 8], [0, 64]], A.is_ge, 0.0, 0, 1), ["eo"], ["gi"])
+    op("gc_", lambda: g.affine_select(T.bo[:], T.gi[:], [[16, 8], [0, 64]], A.is_ge, 0.0, 15, -1), ["gi"], ["bo"])
+    iota(T.iof[:], [[1, C]], -M, 0, "iof")
+    op("gc_", lambda: g.affine_select(T.r0[:], T.eo[:, 0:C], [[0, NC], [1, 16]], A.is_gt, 0.0, 0, 0), ["eo"], ["r0"])
+    ts(T.qi[:], T.pi[:], 15, None, [A.bitwise_and], ["pi"], ["qi"])
+    ts(T.gj[:], T.pi[:], 4, None, [A.arith_shift_right], ["pi"], ["gj"])
+    cp(T.ul[:], T.c8[:], ["c8"], ["ul"])
+    cp(T.qf[:], T.qi[:], ["qi"], ["qf"])
+    cp(T.gf[:], T.gj[:], ["gj"], ["gf"])
     for k, n in enumerate(WIDTH):
         fill(T["bt%d" % k][:, 4 * 16 * (4 * k + 1):4 * n], 0.0, "bz%d" % k)
-    fill(T.wb[:, 16:16 + C], float(C), "wb_a")
-    fill(T.wb[:, 0:16], 0.0, "wb_b")
-    fill(T.wb[:, 16 + C:32 + 2 * C], 0.0, "wb")
-    fill(T.acc[:, 0:1], 0.0, "acc0")
-    iota(T.c8[:], [[16, 8]], 0, 0, "c8")
-    iota(T.pi[:], [[1, 1]], 0, 1, "pi")
-    iota(T.ci[:], [[1, NC]], 0, 0, "ci")
-    iota(T.j16[:], [[0, NC], [1, 16]], 0, 0, "j16")
-    iota(T.gi[:], [[1, 8], [0, 64]], 0, 0, "gi")
-    iota(T.iof[:], [[1, C]], -M, 0, "iof")
-    cp(T.ul[:], T.c8[:], ["c8"], ["ul"])
-    ts(T.qi[:], T.pi[:], 15, None, [A.bitwise_and], ["pi"], ["qi"])
-    ts(T.oi[:], T.pi[:], 16, 4, [A.bitwise_and, A.arith_shift_right], ["pi"], ["oi"])
-    ts(T.gj[:], T.pi[:], 4, None, [A.arith_shift_right], ["pi"], ["gj"])
-    cp(T.qf[:], T.qi[:], ["qi"], ["qf"])
-    tt(T.si[:], T.qi[:], T.oi[:], A.add, ["qi", "oi"], ["si"])
-    ts(T.k2[:], T.qi[:], 16.0, None, [A.mult], ["qi"], ["k2"])
-    cp(T.gf[:], T.gj[:], ["gj"], ["gf"])
-    ts(T.q20[:], T.qf[:], 20.0, None, [A.mult], ["qf"], ["q20"])
-    ts(T.ri[:], T.si[:], 1, None, [A.bitwise_and], ["si"], ["ri"])
-    ts(T.iw[:], T.ci[:], 16.0, T.qf[:, 0:1], [A.mult, A.add], ["ci", "qf"], ["iw"])
-    ts(W["pbf"], T.ci[:], T.q20[:, 0:1], None, [A.add], ["ci", "q20"], ["pbf"])
-    ts(T.k1[:], T.ri[:], float(C + 16), None, [A.mult], ["ri"], ["k1"])
-    ts(T.dlt[:], T.j16[:], T.qf[:, 0:1], None, [A.is_equal], ["j16", "qf"], ["dlt"])
-    ts(T.r0[:], T.j16[:], 0.0, None, [A.is_gt], ["j16"], ["r0"])
-    tt(T.k3[:], T.k1[:], T.k2[:], A.add, ["k1", "k2"], ["k3"])
-    cp(T.pbl[:], W["pbf"], ["pbf"], ["pbl"])
-    ts(T.mk[:], T.dlt[:], -0.5, 2 * BIG, [A.add, A.mult], ["dlt"], ["mk"])
-    ts(T.rs[:], T.r0[:], -0.5, 2 * BIG, [A.add, A.mult], ["r0"], ["rs"])
+
+    def affine(out, a, scale, bias, reads, writes):
+        act(out, a, reads, writes, scale=scale, bias=bias, func=F.Identity)
+
+    def K(i):
+        return T.kk[:, i:i + 1]
+
+    q1 = T.qf[:, 0:1]
+    affine(K(0), q1, 20.0, 0.0, ["qf"], ["k0"])
+    affine(K(1), q1, -1.0, 15.0, ["qf"], ["k1"])
+    affine(K(2), q1, -1.0, 15.0 + 8 * NV, ["qf"], ["k2"])
+    affine(T.acc[:, 0:1], q1, 0.0, 0.0, ["qf"], ["acc0"])
+    act(T.aa[:], T.j16[:], ["j16", "qf"], ["aa"], func=F.Abs, bias=q1, scale=-1.0)
+    affine(T.rs[:], T.j16[:, 0:M], 2 * BIG, -BIG, ["j16"], ["rs"])
+    affine(T.mk[:], T.aa[:, 0:M], -2 * BIG, BIG, ["aa"], ["mk"])
 
     quant(T.uq[:], T.us[:], T.ut[:], ["ut"], ["uq"])
-    cp(T.wl[:, 0:1], T.k3[:], ["k3"], ["wl0"])
+    op("a", lambda: S.activation(T.usr[:, 0:128], T.us[:, 0:128].indirect(T.ul[:, 0:8]), F.Copy), ["uq", "ul"], ["usr"])
+    scores(0, 0, False)
     op("v", lambda: V.tensor_copy(T.uqr[:, 0:128].bitcast(dt.uint32), T.uq[:, 0:128].bitcast(dt.uint32).indirect(T.ul[:, 0:8])), ["uq", "ul"], ["uqr"])
-    op("v", lambda: V.tensor_copy(T.usr[:, 0:128], T.us[:, 0:128].indirect(T.ul[:, 0:8])), ["uq", "ul"], ["usr"])
+    act(T.dlt[:], T.aa[:], ["aa"], ["dlt"], func=F.Relu, bias=1.0, scale=-1.0)
+    affine(T.iw[:], T.ci[:], 16.0, q1, ["ci", "qf"], ["iw"])
+    affine(W["pbf"], T.ci[:], 1.0, K(0), ["ci", "k0"], ["pbf"])
+    affine(T.kr[:, 0:NV + 1], T.ci[:, 0:NV + 1], 0.0, K(2), ["ci", "k2"], ["kr"])
+    affine(T.kr[:, NV + 1:NC], T.ci[:, NV + 1:NC], 16.0, K(1), ["ci", "k1"], ["kr_b"])
 
     def later_constants():
-        ts(T.wl[:, 1:2], T.k3[:], 256.0, float(C + E - 1), [A.add, A.min], ["k3"], ["wl1"])
-        ts(T.bo[:], T.gi[:], T.gf[:, 0:1], None, [A.is_equal], ["gi", "gf"], ["bo"])
-        ts(T.kr[:, 0:NV + 1], T.ci[:, 0:NV + 1], 0.0, 8.0 * NV + 15, [A.mult, A.add], ["ci"], ["kr_a"])
-        ts(T.kr[:, NV + 1:NC], T.ci[:, NV + 1:NC], 16.0, 15.0, [A.mult, A.add], ["ci"], ["kr_b"])
-        quant(T.oq[:], T.os_[:], T.bo[:], ["bo"], ["oq"])
-        ts(T.kr[:], T.kr[:], T.qf[:, 0:1], None, [A.subtract], ["kr_a", "kr_b", "qf"], ["kr"])
+        affine(W["ahi"], T.iw[:], 1.0, C - 0.6, ["iw"], ["ahi"])
+        affine(W["alo"], T.iw[:], 1.0, -0.5, ["iw"], ["alo"])
+        affine(K(3), T.gf[:, 0:1], 1.0, q1, ["gf", "qf"], ["k3"])
+        affine(W["ka"], T.iw[:], -1.0 / C, (M - 0.5) / C, ["iw"], ["ka"])
+        affine(K(4), K(3), 0.5, -0.25, ["k3"], ["k4"])
+        affine(W["ia"], T.iw[:], 1.0 / C, 0.0, ["iw"], ["ia"])
+        affine(K(5), K(4), 1.0, WHOLE, ["k4"], ["k5"])
+        affine(T.wb[:, 16:16 + C], T.eo[:, 0:C], 0.0, float(C), ["eo"], ["wb_a"])
+        affine(K(6), K(5), 1.0, -WHOLE, ["k5"], ["k6"])
+        affine(T.wb[:, 0:16], T.eo[:, 0:16], 0.0, 0.0, ["eo"], ["wb_b"])
+        affine(K(7), K(6), -2.0, K(3), ["k6", "k3"], ["k7"])
+        affine(K(8), q1, 16.0, 0.0, ["qf"], ["k8"])
+        affine(T.wb[:, 16 + C:32 + 2 * C], T.eo[:, 0:C + 16], 0.0, 0.0, ["eo"], ["wb"])
+        affine(K(9), K(7), float(C + 16), K(8), ["k7", "k8"], ["k9"])
 
-    def exchange_constants():
-        ts(W["ahi"], T.iw[:], C - 0.6, None, [A.add], ["iw"], ["ahi"])
-        ts(W["alo"], T.iw[:], -0.5, None, [A.add], ["iw"], ["alo"])
-        ts(W["ka"], T.iw[:], 0.5 - M, -1.0 / C, [A.add, A.mult], ["iw"], ["ka"])
-        ts(W["ia"], T.iw[:], 1.0 / C, None, [A.mult], ["iw"], ["ia"])
+    def unit(t, b):
+        if t == 0:
+            quant(T.eq[:, 128 * b:128 * b + 128], T.es[:, 128 * b:128 * b + 128], T.ee[:, 3 - b:515 - b], ["ee"], ["eq%d" % b])
+
+    def unpack(t):
+        for b in range(4):
+            k = ("ps3", "ps4", "ps0", "ps5")[b]
+            mm(T[k][:, 0:C], T.eq[:, 128 * b:128 * b + 128], T.es[:, 128 * b:128 * b + 128], T["qp%d" % t][:], T["sp%d" % t][:], ["eq%d" % b, "qp%d" % t], [k])
+            act(T.hw[:, 2 * C * b + C:2 * C * b + 2 * C], T[k][:, 0:C], [k], ["d%d" % b], scale=0.5)
 
     def turn(name, at):
         op("v", lambda: V.transpose(T[name][:, 0:C], T.wb[:, at + 16:at + 16 + C]), ["wb"], [name + "a"])
@@ -234,23 +269,20 @@ def rank_program(g, core, T, topo):
     wlk = ["wl0", "wl1"]
     last = slice(15, C, 16)
 
+    def pick(h):
+        k = ("ps6", "ps7")[h]
+        tt(T.m1[:, M * h:M * h + M], T[k][:, M * h:M * h + M], T.mk[:, 0:M], A.min, [k, "mk"], ["m1_%d" % h])
+
+    def hold(h):
+        scan(T.exm[:, M * h:M * h + M], T.rs[:, 0:M], T.m1[:, M * h:M * h + M], [A.min, A.max], ["rs", "m1_%d" % h], ["exm%d" % h])
+
+    mm(T.ps6[:, 0:M], T.uqr[:], T.usr[:], T.qx0[:, 0:M], T.sx0[:, 0:M], ["uqr", "usr", "qx0_0"], ["ps6"])
+    scores(0, 1)
     for t in range(ROUNDS):
-        xt = T.xt0 if t == 0 else T.xt1
-        qx, sx, qk = T["qx%d" % t], T["sx%d" % t], ["qx%d_0" % t, "qx%d_1" % t]
         lw, ln, lk = T["pin" if t == 0 else "lw%d" % t], T["lw%d" % (t + 1)], "lw%d" % t
-        for h in range(2):
-            j = M * h
-            if t and h:
-                ts(xt[:, 4 * M + 3:4 * C:4], T.uu[:, 3 * C + M:4 * C], 2.0 ** -5, None, [A.mult], ["uu3_1"], ["x3_1"])
-            quant(qx[:, j:j + M], sx[:, j:j + M], xt[:, 4 * j:4 * (j + M)], ["x%d_%d" % (b, h) for b in range(4)] if t else ["xt_%d" % h], [qk[h]])
-        uk = ["uqr", "usr"]
-        mm(T.ps6[:, 0:M], T.uqr[:], T.usr[:], qx[:, 0:M], sx[:, 0:M], uk + qk[:1], ["ps6"])
-        mm(T.ps7[:, 0:C], T.uqr[:], T.usr[:], qx[:], sx[:], uk + qk, ["ps7"])
-        mm(T.ps1[:, 0:C], T.uqr[:], T.usr[:], qx[:], sx[:], uk + qk, ["ps1"])
-        send(T["qp%d" % t][:].bitcast(dt.uint8), qx[:].bitcast(dt.uint8), "rq%d" % t, "lq%d" % t, qk)
-        send(T["sp%d" % t][:], sx[:], "rq%d" % t, "lq%d" % t, qk)
         if t == 0:
             op("gc_", lambda: g.affine_select(T.ee[:], T.eo[:], [[1, 516]], A.is_equal, 0.0, -3, -4), ["eo"], ["ee"])
+            iota(T.iob[:], [[1, C]], -M, 0, "iob")
 
         def slot(c):
             k = (c - 1) // 4
@@ -278,6 +310,9 @@ def rank_program(g, core, T, topo):
         def pack(k):
             at, n = sum(WIDTH[:k]), WIDTH[k]
             quant(T.bq[:, at:at + n], T.bs[:, at:at + n], T["bt%d" % k][:], ["b%d" % c for c in range(4 * k + 1, 4 * k + 5)] + ["bz%d" % k], ["bq%d" % k])
+
+        def add(k):
+            at, n = sum(WIDTH[:k]), WIDTH[k]
             mm(T.ps2[:, 0:n], T.oq[:], T.os_[:], T.bq[:, at:at + n], T.bs[:, at:at + n], ["oq", "bq%d" % k], ["ps2"], start=k == 4, stop=k == 0)
 
         def both(cs, bank):
@@ -285,39 +320,50 @@ def rank_program(g, core, T, topo):
                 compare(c, bank)
                 rowsum(c)
 
-        tt(T.m1[:, 0:M], T.ps6[:, 0:M], T.mk[:, 0:M], A.min, ["ps6", "mk"], ["m1_0"])
         if t == 0:
-            later_constants()
-        scan(T.exm[:, 0:M], T.rs[:, 0:M], T.m1[:, 0:M], [A.min, A.max], ["rs", "m1_0"], ["exm0"])
-        tt(T.m1[:, M:C], T.ps7[:, M:C], T.mk[:, 0:M], A.min, ["ps7", "mk"], ["m1_1"])
-        both([8], "ps6")
-        scan(T.exm[:, M:C], T.rs[:, 0:M], T.m1[:, M:C], [A.min, A.max], ["rs", "m1_1"], ["exm1"])
-        compare(7, "ps6")
+            pick(0)
+            cp(T.pbl[:], W["pbf"], ["pbf"], ["pbl"])
+            hold(0)
+        else:
+            both([9, 8, 5, 4], "ps6")
+        pick(1)
+        both([7] if t else [9], "ps6")
+        hold(1)
+        compare(6, "ps6")
         for c in range(NC - 1, NV, -1):
             sign(c)
         for c in range(NC - 1, NV, -1):
             relu(c)
-        rowsum(7)
+        rowsum(6)
+        if t == 0:
+            affine(T.iov[:], T.iof[:], 1.0 / C, 0.5 / C, ["iof"], ["iov"])
         tt(T.bt4[:, 3:4 * C:4], T.ps7[:, 0:C], T.exm[:], A.is_le, ["ps7", "exm0", "exm1", "bz4"], ["b20"])
         both(range(NV, 12, -1), "ps7")
-        pack(4)
+        both([12, 11, 10] if t else [12, 11, 10, 8, 7, 5, 4], "ps7")
+        if t == 0:
+            quant(T.oq[:], T.os_[:], T.bo[:], ["bo"], ["oq"])
         pack(3)
-        both([12, 11, 10, 9, 6, 5], "ps7")
+        pack(4)
+        both([3, 2, 1], "ps7")
         pack(2)
-        both([4, 3, 2, 1], "ps7")
         pack(1)
         pack(0)
+        for k in (4, 3, 2, 1, 0):
+            add(k)
         scan(T.sd[:], T.r0[:], T.bt4[:, 3:4 * C:4], [A.mult, A.add], ["r0", "b20"], ["sd"])
-        ts(W["kb"], lw[:], 1.0 - C, 1.0 / C, [A.add, A.mult], [lk], ["kb"])
-        if t == 0:
-            ts(T.iov[:], T.iof[:], 0.5, 1.0 / C, [A.add, A.mult], ["iof"], ["iov"])
-            cp(T.iob[:], T.iof[:], ["iof"], ["iob"])
-        tt(W["ab"], T.kr[:], T.sd[:, last], A.subtract, ["kr", "sd"], ["ab"])
-        tt(T.ca[:], T.ps2[:, 0:C], T.dlt[:], A.mult, ["ps2", "dlt"], ["ca"])
-        tt(W["ac"], W["ab"], T.acc[:], A.subtract, ["ab"] + ["acc%d" % c for c in range(NC)], ["ac"])
-        scan(T.cs[:], T.r0[:], T.ca[:], [A.mult, A.add], ["r0", "ca"], ["cs"])
         if t == 0:
             tt(T.vb[:], T.pb[:].indirect(T.pbl[:]), T.iov[:], A.add, ["pb", "pbl", "iov"], ["vb"])
+        else:
+            ts(W["kb"], lw[:], 1.0 - C, 1.0 / C, [A.add, A.mult], [lk], ["kb"])
+        tt(W["ab"], T.kr[:], T.sd[:, last], A.subtract, ["kr", "kr_b", "sd"], ["ab"])
+        for j in (0, M):
+            tt(T.ca[:, j:j + M], T.ps2[:, j:j + M], T.dlt[:, 0:M], A.mult, ["ps2", "dlt"], ["ca%d" % j])
+        for j in (0, M):
+            scan(T.cs[:, j:j + M], T.r0[:, 0:M], T.ca[:, j:j + M], [A.mult, A.add], ["r0", "ca%d" % j], ["cs%d" % j])
+        tt(W["ac"], W["ab"], T.acc[:], A.subtract, ["ab"] + ["acc%d" % c for c in range(NC)], ["ac"])
+        unit(t, 0)
+        if t == 0:
+            later_constants()
             act(T.l4[:], T.vb[:], ["vb"], ["l4"], func=F.Identity, bias=WHOLE)
         for dst, w, key in ((T.hw, 2 * C, "h"), (T.hx, C, "g")):
             for b in range(4):
@@ -327,24 +373,23 @@ def rank_program(g, core, T, topo):
                     act(dst[:, w * b:w * b + C], T.uu[:, C * b:C * b + C], ["uu%d_0" % b, "uu%d_1" % b], [key + str(b)], scale=2.0 ** -6)
         if t == 0:
             act(T.l50[:], T.l4[:], ["l4"], ["l50"], func=F.Identity, bias=-WHOLE)
-        tt(W["pli"], W["ac"], T.cs[:, last], A.add, ["ac", "cs"], ["pli"])
-        cp(T.plu[:], W["pli"], ["pli"], ["plu"])
+        tt(W["pli"], W["ac"], T.cs[:, last], A.add, ["ac", "cs0", "cs%d" % M], ["pli"])
+        unit(t, 1)
         ts(W["hh"], W["pli"], -0.5, 0.5, [A.add, A.mult], ["pli"], ["hh"])
         ts(W["pq"], W["pli"], 0.25, None, [A.mult], ["pli"], ["pq"])
-        cp(T.wo[:].indirect(T.plu[:]), T.vb[:], ["plu", "vb"], ["wo"])
+        cp(T.plu[:], W["pli"], ["pli"], ["plu"])
         tt(W["pxi"], W["hh"], W["pq"], A.subtract, ["hh", "pq"], ["pxi"])
-        if t == 0:
-            exchange_constants()
+        cp(T.wo[:].indirect(T.plu[:]), T.vb[:], ["plu", "vb"], ["wo"])
         ts(T.pxu[:], W["pxi"], 4.0, 1.0, [A.mult, A.add], ["pxi"], ["pxu"])
         if t == 0:
-            for b in range(4):
-                quant(T.eq[:, 128 * b:128 * b + 128], T.es[:, 128 * b:128 * b + 128], T.ee[:, 3 - b:515 - b], ["ee"], ["eq%d" % b])
-        for b in range(4):
-            k = ("ps3", "ps4", "ps0", "ps5")[b]
-            mm(T[k][:, 0:C], T.eq[:, 128 * b:128 * b + 128], T.es[:, 128 * b:128 * b + 128], T["qp%d" % t][:], T["sp%d" % t][:], ["eq%d" % b, "qp%d" % t], [k])
-            act(T.hw[:, 2 * C * b + C:2 * C * b + 2 * C], T[k][:, 0:C], [k], ["d%d" % b], scale=0.5)
-        tt(T.gb[:], T.wo[:].indirect(T.pxu[:]), T.dlt[:], A.mult, ["wo", "pxu", "dlt"], ["gb"])
-        scan(T.gs[:], T.r0[:], T.gb[:], [A.mult, A.add], ["r0", "gb"], ["gs"])
+            ts(W["kb"], lw[:], 1.0 - C, 1.0 / C, [A.add, A.mult], [lk], ["kb"])
+        for j in (0, M):
+            tt(T.gb[:, j:j + M], T.wo[:].indirect(T.pxu[:, j // 16:(j + M) // 16]), T.dlt[:, 0:M], A.mult, ["wo", "pxu", "dlt"], ["gb%d" % j])
+        scan(T.gs[:, 0:M], T.r0[:, 0:M], T.gb[:, 0:M], [A.mult, A.add], ["r0", "gb0"], ["gs0"])
+        scan(T.gs[:, M:C], T.r0[:, 0:M], T.gb[:, M:C], [A.mult, A.add], ["r0", "gb%d" % M], ["gs"])
+        unit(t, 2)
+        unit(t, 3)
+        unpack(t)
         v = T.gs[:, last]
         tt(W["lb"], v, W["ahi"], A.min, ["gs", "ahi"], ["lb"])
         tt(W["yi"], v, W["kb"], A.subtract, ["gs", "kb"], ["yi"])
@@ -359,8 +404,12 @@ def rank_program(g, core, T, topo):
         tt(W["bu"], W["bt"], W["ka"], A.add, ["bt", "ka"], ["bu"])
         cp(T.lu[:], ln[:], ["lw%d" % (t + 1)], ["lu"])
         tt(W["pm"], W["mm"], W["bu"], A.mult, ["mm", "bu"], ["pm"])
+        if t == 0:
+            cp(T.wl[:, 0:1], K(9), ["k9"], ["wl0"])
         cp(T.wb[:, 16:16 + 2 * C].indirect(T.lu[:]), T.iob[:], ["lu", "iob", "wb_a"], ["wb"])
         tt(W["pf"], W["pm"], W["ia"], A.add, ["pm", "ia"], ["pf"])
+        if t == 0:
+            ts(T.wl[:, 1:2], K(9), 256.0, float(C + E - 1), [A.add, A.min], ["k9"], ["wl1"])
         turn("tu", C)
         ts(W["pg"], W["pf"], float(C), None, [A.mult], ["pf"], ["pg"])
         up = "up%d" % t
@@ -379,44 +428,61 @@ def rank_program(g, core, T, topo):
         ts(T.lo[:], T.tl[:].indirect(T.wl[:]), float(M), None, [A.add], ["tla", "tlb"] + wlk, ["lo"])
         tt(T.ef[:], T.lo[:, 0:NC], T["la%d" % t][:], A.add, ["lo", "la%d" % t], ["ef"])
         cp(T.eu[:], T.ef[:], ["ef"], ["eu"])
-        for b, h, n in ((0, 0, 2), (1, 0, 2), (2, 0, 2), (3, 0, 1), (3, 1, 1)):
+        banks = (("ps6", "ps7", "ps1", "ps2"), ("ps3", "ps4", "ps0", "ps5"))
+
+        def blend(b, h, n):
             o, j, w = 2 * C * b, M * h, M * n
             zk = ["z%d_%d" % (b, i) for i in range(h, h + n)]
             tt(T.z[:, 4 * j + b:4 * (j + w):4], T.hw[:, o:o + 2 * C].indirect(T.eu[:, j // 16:(j + w) // 16]), T.hx[:, C * b + j:C * b + j + w], A.add,
                ["eu", "h%d" % b, "g%d" % b, "d%d" % b], zk)
             act(T.z32[:, C * b + j:C * b + j + w], T.z[:, 4 * j + b:4 * (j + w):4], zk, ["zz%d_%d" % (b, i) for i in range(h, h + n)], scale=32.0)
-        banks = (("ps6", "ps7", "ps1", "ps2"), ("ps3", "ps4", "ps0", "ps5"))
-        for h in range(2):
+
+        def layer(h):
             j = M * h
             quant(T.zq[:, j:j + M], T.zs[:, j:j + M], T.z[:, 4 * j:4 * (j + M)], ["z%d_%d" % (b, h) for b in range(4)], ["zq%d" % h])
             for b in range(4):
                 k = banks[h][b]
                 mm(T[k][:, 0:M], T.wq[:, 128 * b:128 * b + 128], T.wp[:, 128 * b:128 * b + 128], T.zq[:, j:j + M], T.zs[:, j:j + M], ["w", "zq%d" % h], [k])
-        for h in range(2):
-            j = M * h
-            for b in range(4):
-                k, u = banks[h][b], T.uu[:, C * b + j:C * b + j + M]
-                tt(u, T[k][:, 0:M], T.z32[:, C * b + j:C * b + j + M], A.add, [k, "zz%d_%d" % (b, h)], ["uu%d_%d" % (b, h)])
-                if b < 3:
-                    act(T.xt1[:, 4 * j + b:4 * (j + M):4], u, ["uu%d_%d" % (b, h)], ["x%d_%d" % (b, h)], scale=2.0 ** -5)
-                if (b, h) == (0, 1):
-                    ts(T.xt1[:, 3:4 * M:4], T.uu[:, 3 * C:3 * C + M], 2.0 ** -5, None, [A.mult], ["uu3_0"], ["x3_0"])
 
-    q3, s3 = T["qx%d" % ROUNDS], T["sx%d" % ROUNDS]
-    for h in range(2):
-        j, k = M * h, ("ps6", "ps7")[h]
-        if h:
-            ts(T.xt1[:, 4 * M + 3:4 * C:4], T.uu[:, 3 * C + M:4 * C], 2.0 ** -5, None, [A.mult], ["uu3_1"], ["x3_1"])
-        quant(q3[:, j:j + M], s3[:, j:j + M], T.xt1[:, 4 * j:4 * (j + M)], ["x%d_%d" % (b, h) for b in range(4)], ["q3_%d" % h])
-        mm(T[k][:, 0:M], T.vq[:], T.vs[:], q3[:, j:j + M], s3[:, j:j + M], ["vq", "q3_%d" % h], [k])
-    for h in range(2):
-        j, k = M * h, ("ps6", "ps7")[h]
-        cp(T.yb[:, j:j + M], T[k][:, 0:M], [k], ["yb%d" % h])
-        dma("as"[h], T.y[:, j:j + M], T.yb[:, j:j + M], "dy", ["yb%d" % h], [])
-    qk = ["q3_0", "q3_1"]
-    dma("a", T.oc[:], q3[:].bitcast(dt.uint8), "doc", qk, [])
+        def state(b, h):
+            j = M * h
+            k, u = banks[h][b], T.uu[:, C * b + j:C * b + j + M]
+            tt(u, T[k][:, 0:M], T.z32[:, C * b + j:C * b + j + M], A.add, [k, "zz%d_%d" % (b, h)], ["uu%d_%d" % (b, h)])
+            if b < 3:
+                act(T.xt1[:, 4 * j + b:4 * (j + M):4], u, ["uu%d_%d" % (b, h)], ["x%d_%d" % (b, h)], scale=2.0 ** -5)
+
+        def quarter(h):
+            j = M * h
+            ts(T.xt1[:, 4 * j + 3:4 * (j + M):4], T.uu[:, 3 * C + j:3 * C + j + M], 2.0 ** -5, None, [A.mult], ["uu3_%d" % h], ["x3_%d" % h])
+
+        for b, h, n in ((0, 0, 2), (1, 0, 2), (2, 0, 1), (3, 0, 1), (2, 1, 1)):
+            blend(b, h, n)
+        layer(0)
+        blend(3, 1, 1)
+        state(0, 0)
+        layer(1)
+        for b, h in ((1, 0), (2, 0), (3, 0), (0, 1)):
+            state(b, h)
+        quarter(0)
+        state(1, 1)
+        scores(t + 1, 0)
+        state(2, 1)
+        state(3, 1)
+        if t + 1 < ROUNDS:
+            pick(0)
+        else:
+            cp(T.yb[:, 0:M], T.ps6[:, 0:M], ["ps6"], ["yb0"])
+        quarter(1)
+        if t + 1 < ROUNDS:
+            hold(0)
+        else:
+            dma("a", T.y[:, 0:M], T.yb[:, 0:M], "dy", ["yb0"], [])
+        scores(t + 1, 1)
+
+    cp(T.yb[:, M:C], T.ps7[:, 0:M], ["ps7"], ["yb1"])
     for k in range(4):
-        dma("s" if k % 2 else "a", T.osc[4 * k:4 * k + 4, :], s3[32 * k:32 * k + 4, :], "doc", qk, [])
+        dma("s", T.osc[4 * k:4 * k + 4, :], T.sx3[32 * k:32 * k + 4, :], "doc", ["qx3_0", "qx3_1"], [])
+    dma("a", T.y[:, M:C], T.yb[:, M:C], "dy", ["yb1"], [])
     for t in range(ROUNDS):
         count["rq%d" % t], count["rl%d" % t] = 2 * nmask, nmask
     need("s", [(s, m) for s, m in count.items()])

@@ -6,12 +6,14 @@ C, ROUNDS = 320, 3
 E = C + 32
 M = C // 2
 NC = C // 16
-NS = 3
+NS = 2
 NV = NC - 1 - NS
+EARLY = (9, 8)
 BIG = 2.0 ** 96
 WHOLE = 1.5 * 2.0 ** 23
 F8 = "float8_e4m3fn_x4"
-WIDTH = (128, 128, 192, 256, 320)
+WIDTH = {1: 192, 2: 192, 3: 256, 4: 320}
+SPAN = ((128, C), (0, 128), (448, 192), (640, 256), (896, 320))
 
 SCRATCH = {}
 
@@ -26,30 +28,31 @@ _declare("ut vt gi bo", 512, "bfloat16")
 _declare("eo ee", 516, "bfloat16")
 _declare("hw", 8 * C, "bfloat16")
 _declare("fb", NC * C, "bfloat16")
-_declare("sg", NS * C, "bfloat16")
+_declare("kq", NC, "float32")
 _declare("r0 sd ca cs iob", C, "bfloat16")
 _declare("j16 aa dlt mk rs", M, "bfloat16")
 _declare("wb", 2 * C + 32, "bfloat16")
 _declare("tu tl", C + E, "bfloat16")
-for _k, _n in enumerate(WIDTH):
+for _k, _n in WIDTH.items():
     _declare("bt%d" % _k, 4 * _n, "bfloat16")
-_declare("bq", 1024, F8)
-_declare("bs", 1024, "uint8")
+_declare("bq", sum(SPAN[4]), F8)
+_declare("bs", sum(SPAN[4]), "uint8")
 _declare("uq uqr vq oq", 128, F8)
 _declare("us usr vs os_", 128, "uint8")
 _declare("wq eq", 512, F8)
 _declare("wp es", 512, "uint8")
 _declare("zq qx0 qx1 qx2 qx3 qp0 qp1 qp2", C, F8)
 _declare("zs sx0 sx1 sx2 sx3 sp0 sp1 sp2", C, "uint8")
-_declare("m1 exm vb wo gb gs iof iov yb olb l4 l50 l51 l52", C, "float32")
+_declare("m1 exm vb wo gb gs iof iov yb olb l4 l5", C, "float32")
 _declare("lo", 32, "float32")
 _declare("up0 up1 up2", 32, "bfloat16")
 _declare("la0 la1 la2", NC, "bfloat16")
 _declare("acc kr ci iw ef", NC, "float32")
 _declare("qf gf", 1, "float32")
 _declare("kk", 10, "float32")
-_declare("pin lw1 lw2 lw3", NC, "int32")
-SMALL = {"wf": "ab ac pq pxi kb o1 dl mi o34 md bt bu mm pm pf ahi alo ka ia pbf".split(), "wi": "pli hh lb yi pg".split()}
+_declare("pin", NC, "int32")
+_declare("x0 x1 x2 y1 y2", 3 * NC, "float32")
+SMALL = {"wf": "ab ac pxi kb lr ahi alo pbf".split(), "wi": "pli hh lb yi".split()}
 _declare("wf", NC * len(SMALL["wf"]), "float32")
 _declare("wi", NC * len(SMALL["wi"]), "int32")
 _declare("pb", C, "int32")
@@ -169,7 +172,7 @@ def rank_program(g, core, T, topo):
     for r in range(16):
         dma("s", T.pb[r:128:16, :], T.p[:], "dpb", [], [])
     wrote["pb"] = ("dpb", count["dpb"])
-    dma("s", T.pin[:], T.p[:], "dp", [], ["lw0"])
+    dma("s", T.pin[:], T.p[:], "dp", [], ["pin"])
     dma("s", T.wq[:].bitcast(dt.uint8), T.wc[:], "dw", [], [])
     dma("s", T.wp[:], T.ws[:], "dw", [], ["w"])
     dma("s", T.vt[:], T.v[:], "dv", [], ["vt"])
@@ -187,12 +190,14 @@ def rank_program(g, core, T, topo):
             mm(T[k][:, 0:M], T.vq[:], T.vs[:], qx[:, j:j + M], sx[:, j:j + M], ["vq", qk[h]], [k])
             dma("s", T.oc[:, 4 * j:4 * (j + M)], qx[:, j:j + M].bitcast(dt.uint8), "doc", [qk[h]], [])
         elif h:
+            mm(T.ps3[:, 0:M], T.uqr[:], T.usr[:], qx[:, M:C], sx[:, M:C], uk + qk[1:], ["ps3"])
             mm(T.ps7[:, 0:C], T.uqr[:], T.usr[:], qx[:], sx[:], uk + qk, ["ps7"])
             mm(T.ps1[:, 0:C], T.uqr[:], T.usr[:], qx[:], sx[:], uk + qk, ["ps1"])
             send(T["qp%d" % t][:].bitcast(dt.uint8), qx[:].bitcast(dt.uint8), "rq%d" % t, "lq%d" % t, qk)
             send(T["sp%d" % t][:], sx[:], "rq%d" % t, "lq%d" % t, qk)
         elif product:
-            mm(T.ps6[:, 0:M], T.uqr[:], T.usr[:], qx[:, 0:M], sx[:, 0:M], uk + qk[:1], ["ps6"])
+            for k in ("ps6", "ps2"):
+                mm(T[k][:, 0:M], T.uqr[:], T.usr[:], qx[:, 0:M], sx[:, 0:M], uk + qk[:1], [k])
 
     fill(T.eo[:], 1.0, "eo")
     iota(T.pi[:], [[1, 1]], 0, 1, "pi")
@@ -208,8 +213,8 @@ def rank_program(g, core, T, topo):
     cp(T.ul[:], T.c8[:], ["c8"], ["ul"])
     cp(T.qf[:], T.qi[:], ["qi"], ["qf"])
     cp(T.gf[:], T.gj[:], ["gj"], ["gf"])
-    for k, n in enumerate(WIDTH):
-        fill(T["bt%d" % k][:, 4 * 16 * (4 * k + 1):4 * n], 0.0, "bz%d" % k)
+    for k, n in WIDTH.items():
+        fill(T["bt%d" % k][:, 4 * 16 * (4 * k + 1) if k > 1 else 0:4 * n], 0.0, "bz%d" % k)
 
     def affine(out, a, scale, bias, reads, writes):
         act(out, a, reads, writes, scale=scale, bias=bias, func=F.Identity)
@@ -220,7 +225,6 @@ def rank_program(g, core, T, topo):
     q1 = T.qf[:, 0:1]
     affine(K(0), q1, 20.0, 0.0, ["qf"], ["k0"])
     affine(K(1), q1, -1.0, 15.0, ["qf"], ["k1"])
-    affine(K(2), q1, -1.0, 15.0 + 8 * NV, ["qf"], ["k2"])
     affine(T.acc[:, 0:1], q1, 0.0, 0.0, ["qf"], ["acc0"])
     act(T.aa[:], T.j16[:], ["j16", "qf"], ["aa"], func=F.Abs, bias=q1, scale=-1.0)
     affine(T.rs[:], T.j16[:, 0:M], 2 * BIG, -BIG, ["j16"], ["rs"])
@@ -228,21 +232,27 @@ def rank_program(g, core, T, topo):
 
     quant(T.uq[:], T.us[:], T.ut[:], ["ut"], ["uq"])
     op("a", lambda: S.activation(T.usr[:, 0:128], T.us[:, 0:128].indirect(T.ul[:, 0:8]), F.Copy), ["uq", "ul"], ["usr"])
+    quant(T.bq[:, 192:320], T.bs[:, 192:320], T.bt1[:, 0:512], ["bz1"], ["bqz0"])
     scores(0, 0, False)
     op("v", lambda: V.tensor_copy(T.uqr[:, 0:128].bitcast(dt.uint32), T.uq[:, 0:128].bitcast(dt.uint32).indirect(T.ul[:, 0:8])), ["uq", "ul"], ["uqr"])
     act(T.dlt[:], T.aa[:], ["aa"], ["dlt"], func=F.Relu, bias=1.0, scale=-1.0)
     affine(T.iw[:], T.ci[:], 16.0, q1, ["ci", "qf"], ["iw"])
     affine(W["pbf"], T.ci[:], 1.0, K(0), ["ci", "k0"], ["pbf"])
-    affine(T.kr[:, 0:NV + 1], T.ci[:, 0:NV + 1], 0.0, K(2), ["ci", "k2"], ["kr"])
-    affine(T.kr[:, NV + 1:NC], T.ci[:, NV + 1:NC], 16.0, K(1), ["ci", "k1"], ["kr_b"])
+    runs = ((0, min(EARLY)), (min(EARLY), max(EARLY) + 1), (max(EARLY) + 1, NV + 1), (NV + 1, NC))
+    for i, (a, b) in enumerate(runs):
+        later = sum(1 for c in range(b, NV + 1) if c not in EARLY)
+        affine(T.kq[:, a:b], T.ci[:, a:b], 16.0 * (i % 2), 8.0 * later + (0 if i % 2 else 8.0 * (b - 1)), ["ci"], ["kr%d" % i])
+    affine(T.kr[:], T.kq[:], 1.0, K(1), ["kr%d" % i for i in range(4)] + ["k1"], ["kr"])
+
+    for i in (1, 2):
+        affine(T["x%d" % i][:], T.eo[:, 0:3 * NC], 0.0, 0.0, ["eo"], ["xz%d" % i])
 
     def later_constants():
         affine(W["ahi"], T.iw[:], 1.0, C - 0.6, ["iw"], ["ahi"])
         affine(W["alo"], T.iw[:], 1.0, -0.5, ["iw"], ["alo"])
         affine(K(3), T.gf[:, 0:1], 1.0, q1, ["gf", "qf"], ["k3"])
-        affine(W["ka"], T.iw[:], -1.0 / C, (M - 0.5) / C, ["iw"], ["ka"])
+        affine(T.x0[:], T.eo[:, 0:3 * NC], 0.0, 0.0, ["eo"], ["xz0"])
         affine(K(4), K(3), 0.5, -0.25, ["k3"], ["k4"])
-        affine(W["ia"], T.iw[:], 1.0 / C, 0.0, ["iw"], ["ia"])
         affine(K(5), K(4), 1.0, WHOLE, ["k4"], ["k5"])
         affine(T.wb[:, 16:16 + C], T.eo[:, 0:C], 0.0, float(C), ["eo"], ["wb_a"])
         affine(K(6), K(5), 1.0, -WHOLE, ["k5"], ["k6"])
@@ -270,23 +280,24 @@ def rank_program(g, core, T, topo):
     last = slice(15, C, 16)
 
     def pick(h):
-        k = ("ps6", "ps7")[h]
-        tt(T.m1[:, M * h:M * h + M], T[k][:, M * h:M * h + M], T.mk[:, 0:M], A.min, [k, "mk"], ["m1_%d" % h])
+        k = ("ps6", "ps3")[h]
+        tt(T.m1[:, M * h:M * h + M], T[k][:, 0:M], T.mk[:, 0:M], A.min, [k, "mk"], ["m1_%d" % h])
 
     def hold(h):
         scan(T.exm[:, M * h:M * h + M], T.rs[:, 0:M], T.m1[:, M * h:M * h + M], [A.min, A.max], ["rs", "m1_%d" % h], ["exm%d" % h])
 
-    mm(T.ps6[:, 0:M], T.uqr[:], T.usr[:], T.qx0[:, 0:M], T.sx0[:, 0:M], ["uqr", "usr", "qx0_0"], ["ps6"])
+    for k in ("ps6", "ps2"):
+        mm(T[k][:, 0:M], T.uqr[:], T.usr[:], T.qx0[:, 0:M], T.sx0[:, 0:M], ["uqr", "usr", "qx0_0"], [k])
     scores(0, 1)
     for t in range(ROUNDS):
-        lw, ln, lk = T["pin" if t == 0 else "lw%d" % t], T["lw%d" % (t + 1)], "lw%d" % t
+        lw = T.x1[:, 2::3]
         if t == 0:
             op("gc_", lambda: g.affine_select(T.ee[:], T.eo[:], [[1, 516]], A.is_equal, 0.0, -3, -4), ["eo"], ["ee"])
             iota(T.iob[:], [[1, C]], -M, 0, "iob")
 
         def slot(c):
-            k = (c - 1) // 4
-            return T["bt%d" % k][:, (c - 1) % 4:4 * 16 * c:4], "b%d" % c
+            k, at = ((c - 1) // 4, 0) if c > 4 else (1, 4 * 128)
+            return T["bt%d" % k][:, at + (c - 1) % 4:at + 4 * 16 * c:4], "b%d" % c
 
         def own(c):
             return T.exm[:, 16 * c + 15:16 * c + 16], "exm%d" % (16 * c // M)
@@ -301,19 +312,20 @@ def rank_program(g, core, T, topo):
 
         def sign(c):
             s, sk = own(c)
-            act(T.sg[:, C * (c - NV - 1):C * (c - NV - 1) + 16 * c], T.ps1[:, 0:16 * c], ["ps1", sk], ["sg%d" % c], scale=-1.0, bias=s, func=F.Sign)
+            bank = "ps2" if c in EARLY else "ps1"
+            act(T.fb[:, C * c:C * c + 16 * c], T[bank][:, 0:16 * c], [bank, sk], ["sg%d" % c], scale=-1.0, bias=s, func=F.Sign)
 
         def relu(c):
             o, k = slot(c)
-            act(o, T.sg[:, C * (c - NV - 1):C * (c - NV - 1) + 16 * c], ["sg%d" % c], [k, "acc%d" % c], func=F.Relu, accum=T.acc[:, c:c + 1])
+            act(o, T.fb[:, C * c:C * c + 16 * c], ["sg%d" % c], [k, "acc%d" % c], func=F.Relu, accum=T.acc[:, c:c + 1])
 
         def pack(k):
-            at, n = sum(WIDTH[:k]), WIDTH[k]
-            quant(T.bq[:, at:at + n], T.bs[:, at:at + n], T["bt%d" % k][:], ["b%d" % c for c in range(4 * k + 1, 4 * k + 5)] + ["bz%d" % k], ["bq%d" % k])
+            at, n = SPAN[k][0], WIDTH[k]
+            quant(T.bq[:, at:at + n], T.bs[:, at:at + n], T["bt%d" % k][:], ["b%d" % c for c in range(4 * k + 1 if k > 1 else 1, 4 * k + 5)] + ["bz%d" % k], ["bq%d" % k])
 
         def add(k):
-            at, n = sum(WIDTH[:k]), WIDTH[k]
-            mm(T.ps2[:, 0:n], T.oq[:], T.os_[:], T.bq[:, at:at + n], T.bs[:, at:at + n], ["oq", "bq%d" % k], ["ps2"], start=k == 4, stop=k == 0)
+            at, n = SPAN[k]
+            mm(T.ps2[:, 0:n], T.oq[:], T.os_[:], T.bq[:, at:at + n], T.bs[:, at:at + n], ["oq", "bq%d" % max(k, 1), "bqz0", "bqz1"], ["ps2"], start=k == 0, stop=k == 2)
 
         def both(cs, bank):
             for c in cs:
@@ -321,68 +333,73 @@ def rank_program(g, core, T, topo):
                 rowsum(c)
 
         if t == 0:
+            quant(T.bq[:, 320:448], T.bs[:, 320:448], T.bt1[:, 0:512], ["bz1"], ["bqz1"])
             pick(0)
             cp(T.pbl[:], W["pbf"], ["pbf"], ["pbl"])
             hold(0)
-        else:
-            both([9, 8, 5, 4], "ps6")
+        for step in (sign, relu):
+            for c in EARLY:
+                step(c)
+        if t:
+            both([4, 3, 2, 1, 7, 6], "ps6")
         pick(1)
-        both([7] if t else [9], "ps6")
+        both([5], "ps6")
         hold(1)
-        compare(6, "ps6")
-        for c in range(NC - 1, NV, -1):
-            sign(c)
-        for c in range(NC - 1, NV, -1):
-            relu(c)
-        rowsum(6)
+        if t:
+            pack(1)
+        else:
+            for c in (7, 6):
+                compare(c, "ps6")
+        for step in (sign, relu):
+            for c in range(NC - 1, NV, -1):
+                step(c)
         if t == 0:
+            rowsum(7)
+            rowsum(6)
             affine(T.iov[:], T.iof[:], 1.0 / C, 0.5 / C, ["iof"], ["iov"])
         tt(T.bt4[:, 3:4 * C:4], T.ps7[:, 0:C], T.exm[:], A.is_le, ["ps7", "exm0", "exm1", "bz4"], ["b20"])
-        both(range(NV, 12, -1), "ps7")
-        both([12, 11, 10] if t else [12, 11, 10, 8, 7, 5, 4], "ps7")
+        both(range(NV, 9, -1), "ps7")
         if t == 0:
+            both([4, 3, 2, 1], "ps7")
             quant(T.oq[:], T.os_[:], T.bo[:], ["bo"], ["oq"])
-        pack(3)
-        pack(4)
-        both([3, 2, 1], "ps7")
-        pack(2)
-        pack(1)
-        pack(0)
-        for k in (4, 3, 2, 1, 0):
+            pack(1)
+        for k in (3, 4, 2):
+            pack(k)
+        for k in (0, 1, 3, 4, 2):
             add(k)
         scan(T.sd[:], T.r0[:], T.bt4[:, 3:4 * C:4], [A.mult, A.add], ["r0", "b20"], ["sd"])
         if t == 0:
             tt(T.vb[:], T.pb[:].indirect(T.pbl[:]), T.iov[:], A.add, ["pb", "pbl", "iov"], ["vb"])
-        else:
-            ts(W["kb"], lw[:], 1.0 - C, 1.0 / C, [A.add, A.mult], [lk], ["kb"])
-        tt(W["ab"], T.kr[:], T.sd[:, last], A.subtract, ["kr", "kr_b", "sd"], ["ab"])
+        tt(W["ab"], T.kr[:], T.sd[:, last], A.subtract, ["kr", "sd"], ["ab"])
         for j in (0, M):
             tt(T.ca[:, j:j + M], T.ps2[:, j:j + M], T.dlt[:, 0:M], A.mult, ["ps2", "dlt"], ["ca%d" % j])
         for j in (0, M):
             scan(T.cs[:, j:j + M], T.r0[:, 0:M], T.ca[:, j:j + M], [A.mult, A.add], ["r0", "ca%d" % j], ["cs%d" % j])
-        tt(W["ac"], W["ab"], T.acc[:], A.subtract, ["ab"] + ["acc%d" % c for c in range(NC)], ["ac"])
+            if j == 0:
+                tt(W["ac"], W["ab"], T.acc[:], A.subtract, ["ab"] + ["acc%d" % c for c in range(NC)], ["ac"])
         unit(t, 0)
         if t == 0:
+            cp(lw, T.pin[:], ["pin", "xz1"], ["lw"])
+            affine(W["kb"], lw, 1.0 / C, (1.0 - C) / C, ["lw"], ["kb"])
             later_constants()
-            act(T.l4[:], T.vb[:], ["vb"], ["l4"], func=F.Identity, bias=WHOLE)
         for dst, w, key in ((T.hw, 2 * C, "h"), (T.hx, C, "g")):
             for b in range(4):
                 if t == 0:
                     act(dst[:, w * b:w * b + C], T.xt0[:, b:4 * C:4], ["xt_0", "xt_1"], [key + str(b)], scale=0.5)
                 else:
                     act(dst[:, w * b:w * b + C], T.uu[:, C * b:C * b + C], ["uu%d_0" % b, "uu%d_1" % b], [key + str(b)], scale=2.0 ** -6)
-        if t == 0:
-            act(T.l50[:], T.l4[:], ["l4"], ["l50"], func=F.Identity, bias=-WHOLE)
         tt(W["pli"], W["ac"], T.cs[:, last], A.add, ["ac", "cs0", "cs%d" % M], ["pli"])
         unit(t, 1)
+        pq = T.x2[:, 2::3]
         ts(W["hh"], W["pli"], -0.5, 0.5, [A.add, A.mult], ["pli"], ["hh"])
-        ts(W["pq"], W["pli"], 0.25, None, [A.mult], ["pli"], ["pq"])
+        ts(pq, W["pli"], -0.5, 0.25, [A.add, A.mult], ["pli", "xz2"], ["pq"])
         cp(T.plu[:], W["pli"], ["pli"], ["plu"])
-        tt(W["pxi"], W["hh"], W["pq"], A.subtract, ["hh", "pq"], ["pxi"])
+        tt(W["pxi"], W["hh"], pq, A.subtract, ["hh", "pq"], ["pxi"])
         cp(T.wo[:].indirect(T.plu[:]), T.vb[:], ["plu", "vb"], ["wo"])
-        ts(T.pxu[:], W["pxi"], 4.0, 1.0, [A.mult, A.add], ["pxi"], ["pxu"])
-        if t == 0:
-            ts(W["kb"], lw[:], 1.0 - C, 1.0 / C, [A.add, A.mult], [lk], ["kb"])
+        ts(T.pxu[:], W["pxi"], 4.0, 0.5, [A.mult, A.add], ["pxi"], ["pxu"])
+        tt(T.x2[:, 0::3], W["pxi"], pq, A.subtract, ["pxi", "pq"], ["dd"])
+        affine(T.l4[:], T.wo[:], 1.0, WHOLE, ["wo"], ["l4"])
+        affine(T.l5[:], T.l4[:], 1.0, -WHOLE, ["l4"], ["l5"])
         for j in (0, M):
             tt(T.gb[:, j:j + M], T.wo[:].indirect(T.pxu[:, j // 16:(j + M) // 16]), T.dlt[:, 0:M], A.mult, ["wo", "pxu", "dlt"], ["gb%d" % j])
         scan(T.gs[:, 0:M], T.r0[:, 0:M], T.gb[:, 0:M], [A.mult, A.add], ["r0", "gb0"], ["gs0"])
@@ -393,36 +410,30 @@ def rank_program(g, core, T, topo):
         v = T.gs[:, last]
         tt(W["lb"], v, W["ahi"], A.min, ["gs", "ahi"], ["lb"])
         tt(W["yi"], v, W["kb"], A.subtract, ["gs", "kb"], ["yi"])
-        tt(W["o1"], v, W["alo"], A.is_ge, ["gs", "alo"], ["o1"])
-        tt(W["dl"], v, lw[:], A.subtract, ["gs", lk], ["dl"])
-        tt(W["o34"], W["yi"], W["lb"], A.is_equal, ["yi", "lb"], ["o34"])
-        tt(W["mi"], W["o1"], W["dl"], A.mult, ["o1", "dl"], ["mi"])
-        tt(W["bt"], v, W["lb"], A.subtract, ["gs", "lb"], ["bt"])
-        tt(W["md"], W["mi"], W["o34"], A.mult, ["mi", "o34"], ["md"])
-        tt(W["mm"], W["o1"], W["o34"], A.mult, ["o1", "o34"], ["mm"])
-        tt(ln[:], lw[:], W["md"], A.add, [lk, "md"], ["lw%d" % (t + 1)])
-        tt(W["bu"], W["bt"], W["ka"], A.add, ["bt", "ka"], ["bu"])
-        cp(T.lu[:], ln[:], ["lw%d" % (t + 1)], ["lu"])
-        tt(W["pm"], W["mm"], W["bu"], A.mult, ["mm", "bu"], ["pm"])
+        tt(T.x0[:, 1::3], v, W["alo"], A.is_ge, ["gs", "alo", "xz0"], ["o1"])
+        tt(T.x1[:, 0::3], v, lw, A.subtract, ["gs", "lw"], ["dl"])
+        tt(T.x0[:, 2::3], W["yi"], W["lb"], A.is_equal, ["yi", "lb"], ["o34"])
         if t == 0:
             cp(T.wl[:, 0:1], K(9), ["k9"], ["wl0"])
-        cp(T.wb[:, 16:16 + 2 * C].indirect(T.lu[:]), T.iob[:], ["lu", "iob", "wb_a"], ["wb"])
-        tt(W["pf"], W["pm"], W["ia"], A.add, ["pm", "ia"], ["pf"])
-        if t == 0:
             ts(T.wl[:, 1:2], K(9), 256.0, float(C + E - 1), [A.add, A.min], ["k9"], ["wl1"])
+        scan(T.y1[:], T.x0[:], T.x1[:], [A.mult, A.add], ["o1", "o34", "dl", "lw"], ["y1"])
+        scan(T.y2[:], T.x0[:], T.x2[:], [A.mult, A.add], ["o1", "o34", "dd", "pq"], ["y2"])
+        ts(T.lu[:], T.y1[:, 2::3], WHOLE, -WHOLE, [A.add, A.add], ["y1"], ["lu"])
+        ts(T.pu[:], T.y2[:, 2::3], 4.0, 0.5, [A.mult, A.add], ["y2"], ["pu"])
+        if t + 1 < ROUNDS:
+            affine(W["lr"], T.y1[:, 2::3], 1.0, WHOLE, ["y1"], ["lr"])
+            affine(lw, W["lr"], 1.0, -WHOLE, ["lr"], ["lw"])
+            affine(W["kb"], lw, 1.0 / C, (1.0 - C) / C, ["lw"], ["kb"])
+        cp(T.wb[:, 16:16 + 2 * C].indirect(T.lu[:]), T.iob[:], ["lu", "iob", "wb_a"], ["wb"])
         turn("tu", C)
-        ts(W["pg"], W["pf"], float(C), None, [A.mult], ["pf"], ["pg"])
         up = "up%d" % t
         cp(T[up][:], T.tu[:].indirect(T.wl[:]), ["tua", "tub"] + wlk, [up])
         send(T["la%d" % t][:], T[up][:, 0:NC], "rl%d" % t, "ll%d" % t, [up])
-        cp(T.pu[:], W["pg"], ["pg"], ["pu"])
         turn("tl", 0)
-        l5, l5k = T["l5%d" % t], "l5%d" % t
         if t + 1 < ROUNDS:
-            act(T["l5%d" % (t + 1)][:], l5[:].indirect(T.pu[:]), [l5k, "pu"], ["l5%d" % (t + 1)])
-            tt(T.vb[:], l5[:].indirect(T.pu[:]), T.iov[:], A.add, [l5k, "pu", "iov"], ["vb"])
+            tt(T.vb[:], T.l5[:].indirect(T.pu[:]), T.iov[:], A.add, ["l5", "pu", "iov"], ["vb"])
         else:
-            act(T.olb[:], l5[:].indirect(T.pu[:]), [l5k, "pu"], ["olb"])
+            act(T.olb[:], T.l5[:].indirect(T.pu[:]), ["l5", "pu"], ["olb"])
             dma("s", T.ol[:], T.olb[0:128:16, :], "dol", ["olb"], [])
             quant(T.vq[:], T.vs[:], T.vt[:], ["vt"], ["vq"])
         ts(T.lo[:], T.tl[:].indirect(T.wl[:]), float(M), None, [A.add], ["tla", "tlb"] + wlk, ["lo"])
@@ -444,20 +455,21 @@ def rank_program(g, core, T, topo):
                 k = banks[h][b]
                 mm(T[k][:, 0:M], T.wq[:, 128 * b:128 * b + 128], T.wp[:, 128 * b:128 * b + 128], T.zq[:, j:j + M], T.zs[:, j:j + M], ["w", "zq%d" % h], [k])
 
-        def state(b, h):
+        def state(b, h, scaled=True):
             j = M * h
             k, u = banks[h][b], T.uu[:, C * b + j:C * b + j + M]
             tt(u, T[k][:, 0:M], T.z32[:, C * b + j:C * b + j + M], A.add, [k, "zz%d_%d" % (b, h)], ["uu%d_%d" % (b, h)])
-            if b < 3:
+            if b < 3 and scaled:
                 act(T.xt1[:, 4 * j + b:4 * (j + M):4], u, ["uu%d_%d" % (b, h)], ["x%d_%d" % (b, h)], scale=2.0 ** -5)
 
-        def quarter(h):
+        def quarter(h, b=3):
             j = M * h
-            ts(T.xt1[:, 4 * j + 3:4 * (j + M):4], T.uu[:, 3 * C + j:3 * C + j + M], 2.0 ** -5, None, [A.mult], ["uu3_%d" % h], ["x3_%d" % h])
+            ts(T.xt1[:, 4 * j + b:4 * (j + M):4], T.uu[:, b * C + j:b * C + j + M], 2.0 ** -5, None, [A.mult], ["uu%d_%d" % (b, h)], ["x%d_%d" % (b, h)])
 
-        for b, h, n in ((0, 0, 2), (1, 0, 2), (2, 0, 1), (3, 0, 1), (2, 1, 1)):
+        for b, h, n in ((0, 0, 2), (1, 0, 1), (2, 0, 1), (3, 0, 1), (1, 1, 1)):
             blend(b, h, n)
         layer(0)
+        blend(2, 1, 1)
         blend(3, 1, 1)
         state(0, 0)
         layer(1)
@@ -466,16 +478,18 @@ def rank_program(g, core, T, topo):
         quarter(0)
         state(1, 1)
         scores(t + 1, 0)
-        state(2, 1)
-        state(3, 1)
         if t + 1 < ROUNDS:
+            state(2, 1)
+            state(3, 1)
             pick(0)
-        else:
-            cp(T.yb[:, 0:M], T.ps6[:, 0:M], ["ps6"], ["yb0"])
-        quarter(1)
-        if t + 1 < ROUNDS:
+            quarter(1)
             hold(0)
         else:
+            state(2, 1, False)
+            state(3, 1)
+            quarter(1, 2)
+            quarter(1)
+            act(T.yb[:, 0:M], T.ps6[:, 0:M], ["ps6"], ["yb0"])
             dma("a", T.y[:, 0:M], T.yb[:, 0:M], "dy", ["yb0"], [])
         scores(t + 1, 1)
 

from concourse.mybir import dt, AluOpType, ActivationFunctionType

A = AluOpType
F = ActivationFunctionType
C, ROUNDS = 320, 3
E = C + 32
M = C // 2
NC = C // 16
NS = 2
NV = NC - 1 - NS
EARLY = (9, 8)
BIG = 2.0 ** 96
WHOLE = 1.5 * 2.0 ** 23
F8 = "float8_e4m3fn_x4"
WIDTH = {1: 192, 2: 192, 3: 256, 4: 320}
SPAN = ((128, C), (0, 128), (448, 192), (640, 256), (896, 320))

SCRATCH = {}


def _declare(names, columns, dtype, where="sbuf"):
    for name in names.split():
        SCRATCH[name] = (where, [128, columns], dtype)


_declare("xt0 xt1 z z32 uu hx", 4 * C, "bfloat16")
_declare("ut vt gi bo", 512, "bfloat16")
_declare("eo ee", 516, "bfloat16")
_declare("hw", 8 * C, "bfloat16")
_declare("fb", NC * C, "bfloat16")
_declare("kq", NC, "float32")
_declare("r0 sd ca cs iob", C, "bfloat16")
_declare("j16 aa dlt mk rs", M, "bfloat16")
_declare("wb", 2 * C + 32, "bfloat16")
_declare("tu tl", C + E, "bfloat16")
for _k, _n in WIDTH.items():
    _declare("bt%d" % _k, 4 * _n, "bfloat16")
_declare("bq", sum(SPAN[4]), F8)
_declare("bs", sum(SPAN[4]), "uint8")
_declare("uq uqr vq oq", 128, F8)
_declare("us usr vs os_", 128, "uint8")
_declare("wq eq", 512, F8)
_declare("wp es", 512, "uint8")
_declare("zq qx0 qx1 qx2 qx3 qp0 qp1 qp2", C, F8)
_declare("zs sx0 sx1 sx2 sx3 sp0 sp1 sp2", C, "uint8")
_declare("m1 exm vb wo gb gs iof iov yb olb l4 l5", C, "float32")
_declare("lo", 32, "float32")
_declare("up0 up1 up2", 32, "bfloat16")
_declare("la0 la1 la2", NC, "bfloat16")
_declare("acc kr ci iw ef", NC, "float32")
_declare("qf gf", 1, "float32")
_declare("kk", 10, "float32")
_declare("pin", NC, "int32")
_declare("x0 x1 x2 y1 y2", 3 * NC, "float32")
SMALL = {"wf": "ab ac pxi kb lr ahi alo pbf".split(), "wi": "pli hh lb yi".split()}
_declare("wf", NC * len(SMALL["wf"]), "float32")
_declare("wi", NC * len(SMALL["wi"]), "int32")
_declare("pb", C, "int32")
_declare("c8", 8, "int32")
_declare("pi qi gj", 1, "int32")
_declare("plu pxu pu pbl lu eu", NC, "uint16")
_declare("ul", 8, "uint16")
_declare("wl", 2, "uint16")
_declare("ps0 ps1 ps2 ps3 ps4 ps5 ps6 ps7", 512, "float32", "psum")

SEMAPHORES = (["v", "a", "t", "gc_", "dx0", "dx1", "du", "dp", "dpb", "dw", "dv", "dy", "dol", "doc"]
              + ["%s%d" % (n, t) for n in ("rq", "rl", "lq", "ll") for t in range(ROUNDS)])


def rank_program(g, core, T, topo):
    rank = T.rank_of(core)
    if rank is None:
        return
    nxt = T.cores[(rank + 1) % len(T.cores)]
    rid, pid = topo.addr(nxt)[:2]
    mask = topo.mask(core, nxt)
    nmask = len(topo.engines(core, nxt))
    eng = {"v": g.vector, "a": g.scalar, "t": g.tensor, "gc_": g, "s": g.sync}

    count, known, snap = {}, {q: {} for q in eng}, {}
    wrote, read, order = {}, {}, [0]

    def need(q, toks):
        for k in sorted(set(toks), key=lambda k: (snap.get(k, (0, {}))[0], k), reverse=True):
            if known[q].get(k[0], 0) >= k[1]:
                continue
            eng[q].wait_ge(T.sem[k[0]], k[1])
            for s, m in list(snap.get(k, (0, {}))[1].items()) + [k]:
                if known[q].get(s, 0) < m:
                    known[q][s] = m

    def deps(q, reads, writes):
        toks = []
        for k in reads:
            if k in wrote:
                toks.append(wrote[k])
            if k[:2] == "ps":
                toks += [(s, m) for s, m in read.get(k, {}).items() if s != q]
        for k in writes:
            if k in wrote:
                toks.append(wrote[k])
            toks += [(s, m) for s, m in read.get(k, {}).items() if s != q]
        return toks

    def note(tok, reads, writes, q):
        order[0] += 1
        snap[tok] = (order[0], dict(known[q]))
        for k in reads:
            read.setdefault(k, {})[tok[0]] = tok[1]
        for k in writes:
            wrote[k] = tok
            read[k] = {}

    def op(q, fn, reads, writes, free=()):
        need(q, [k for k in deps(q, reads, writes) if k not in free])
        fn().then_inc(T.sem[q], 1)
        count[q] = count.get(q, 0) + 1
        note((q, count[q]), reads, writes, q)

    def dma(q, out, in_, sem, reads, writes):
        need(q, deps(q, reads, writes))
        eng[q].dma_start(out, in_).then_inc(T.sem[sem], 16)
        count[sem] = count.get(sem, 0) + 16
        note((sem, count[sem]), reads, writes, q)

    def send(out, in_, rsem, lsem, reads):
        need("gc_", deps("gc_", reads, []))
        g.remote_dma(out, in_, T.sem[rsem], T.sem[lsem], pid, rid, mask)
        count[lsem] = count.get(lsem, 0) + nmask

    V, S, P = g.vector, g.scalar, g.tensor
    W = {n: T[b][:, NC * i:NC * i + NC] for b, names in SMALL.items() for i, n in enumerate(names)}

    def tt(out, a, b, o, reads, writes):
        op("v", lambda: V.tensor_tensor(out, a, b, o), reads, writes)

    def ts(out, a, s1, s2, o, reads, writes):
        if len(o) == 1:
            op("v", lambda: V.tensor_scalar(out, a, s1, None, o[0]), reads, writes)
        else:
            op("v", lambda: V.tensor_scalar(out, a, s1, s2, o[0], o[1]), reads, writes)

    def cp(out, a, reads, writes):
        op("v", lambda: V.tensor_copy(out, a), reads, writes)

    def scan(out, a, b, o, reads, writes):
        op("v", lambda: V.tensor_tensor_scan(out, a, b, 0.0, o[0], o[1]), reads, writes)

    def fill(out, value, key):
        op("v", lambda: V.memset(out, value), [], [key])

    def act(out, a, reads, writes, scale=1.0, accum=None, func=F.Copy, bias=None):
        if bias is None:
            op("a", lambda: S.activation(out, a, func, scale=scale, accum_out=accum), reads, writes)
        else:
            op("a", lambda: S.activation(out, a, func, bias=bias, scale=scale, accum_out=accum), reads, writes)

    def quant(q, s, a, reads, writes):
        op("v", lambda: V.quantize_mx(q, s, a), reads, writes)

    def mm(out, lq, ls, rq, rs, reads, writes, start=True, stop=True):
        free = () if start else [wrote[k] for k in writes]
        op("t", lambda: P.matmul_mx(out, lq, ls, rq, rs, start, stop), reads, writes, free)

    for t in range(ROUNDS):
        wrote["qp%d" % t] = ("rq%d" % t, 2 * nmask)
        wrote["la%d" % t] = ("rl%d" % t, nmask)

    dma("a", T.ut[:], T.u[:], "du", [], ["ut"])
    dma("s", T.xt0[:, 0:4 * M], T.x[:, 0:4 * M], "dx0", [], ["xt_0"])
    dma("s", T.xt0[:, 4 * M:4 * C], T.x[:, 4 * M:4 * C], "dx1", [], ["xt_1"])
    for r in range(16):
        dma("s", T.pb[r:128:16, :], T.p[:], "dpb", [], [])
    wrote["pb"] = ("dpb", count["dpb"])
    dma("s", T.pin[:], T.p[:], "dp", [], ["pin"])
    dma("s", T.wq[:].bitcast(dt.uint8), T.wc[:], "dw", [], [])
    dma("s", T.wp[:], T.ws[:], "dw", [], ["w"])
    dma("s", T.vt[:], T.v[:], "dv", [], ["vt"])

    def iota(out, pattern, base, mul, key):
        op("gc_", lambda: g.iota(out, pattern, base, mul, allow_small_or_imprecise_dtypes=True), [], [key])

    def scores(t, h, product=True):
        xt = T.xt0 if t == 0 else T.xt1
        qx, sx, qk = T["qx%d" % t], T["sx%d" % t], ["qx%d_0" % t, "qx%d_1" % t]
        j, uk = M * h, ["uqr", "usr"]
        quant(qx[:, j:j + M], sx[:, j:j + M], xt[:, 4 * j:4 * (j + M)], ["x%d_%d" % (b, h) for b in range(4)] if t else ["xt_%d" % h], [qk[h]])
        if t == ROUNDS:
            k = ("ps6", "ps7")[h]
            mm(T[k][:, 0:M], T.vq[:], T.vs[:], qx[:, j:j + M], sx[:, j:j + M], ["vq", qk[h]], [k])
            dma("s", T.oc[:, 4 * j:4 * (j + M)], qx[:, j:j + M].bitcast(dt.uint8), "doc", [qk[h]], [])
        elif h:
            mm(T.ps3[:, 0:M], T.uqr[:], T.usr[:], qx[:, M:C], sx[:, M:C], uk + qk[1:], ["ps3"])
            mm(T.ps7[:, 0:C], T.uqr[:], T.usr[:], qx[:], sx[:], uk + qk, ["ps7"])
            mm(T.ps1[:, 0:C], T.uqr[:], T.usr[:], qx[:], sx[:], uk + qk, ["ps1"])
            send(T["qp%d" % t][:].bitcast(dt.uint8), qx[:].bitcast(dt.uint8), "rq%d" % t, "lq%d" % t, qk)
            send(T["sp%d" % t][:], sx[:], "rq%d" % t, "lq%d" % t, qk)
        elif product:
            for k in ("ps6", "ps2"):
                mm(T[k][:, 0:M], T.uqr[:], T.usr[:], qx[:, 0:M], sx[:, 0:M], uk + qk[:1], [k])

    fill(T.eo[:], 1.0, "eo")
    iota(T.pi[:], [[1, 1]], 0, 1, "pi")
    iota(T.c8[:], [[16, 8]], 0, 0, "c8")
    iota(T.j16[:], [[0, M // 16], [1, 16]], 0, 0, "j16")
    iota(T.ci[:], [[1, NC]], 0, 0, "ci")
    op("gc_", lambda: g.affine_select(T.gi[:], T.eo[:, 0:512], [[-16, 8], [0, 64]], A.is_ge, 0.0, 0, 1), ["eo"], ["gi"])
    op("gc_", lambda: g.affine_select(T.bo[:], T.gi[:], [[16, 8], [0, 64]], A.is_ge, 0.0, 15, -1), ["gi"], ["bo"])
    iota(T.iof[:], [[1, C]], -M, 0, "iof")
    op("gc_", lambda: g.affine_select(T.r0[:], T.eo[:, 0:C], [[0, NC], [1, 16]], A.is_gt, 0.0, 0, 0), ["eo"], ["r0"])
    ts(T.qi[:], T.pi[:], 15, None, [A.bitwise_and], ["pi"], ["qi"])
    ts(T.gj[:], T.pi[:], 4, None, [A.arith_shift_right], ["pi"], ["gj"])
    cp(T.ul[:], T.c8[:], ["c8"], ["ul"])
    cp(T.qf[:], T.qi[:], ["qi"], ["qf"])
    cp(T.gf[:], T.gj[:], ["gj"], ["gf"])
    for k, n in WIDTH.items():
        fill(T["bt%d" % k][:, 4 * 16 * (4 * k + 1) if k > 1 else 0:4 * n], 0.0, "bz%d" % k)

    def affine(out, a, scale, bias, reads, writes):
        act(out, a, reads, writes, scale=scale, bias=bias, func=F.Identity)

    def K(i):
        return T.kk[:, i:i + 1]

    q1 = T.qf[:, 0:1]
    affine(K(0), q1, 20.0, 0.0, ["qf"], ["k0"])
    affine(K(1), q1, -1.0, 15.0, ["qf"], ["k1"])
    affine(T.acc[:, 0:1], q1, 0.0, 0.0, ["qf"], ["acc0"])
    act(T.aa[:], T.j16[:], ["j16", "qf"], ["aa"], func=F.Abs, bias=q1, scale=-1.0)
    affine(T.rs[:], T.j16[:, 0:M], 2 * BIG, -BIG, ["j16"], ["rs"])
    affine(T.mk[:], T.aa[:, 0:M], -2 * BIG, BIG, ["aa"], ["mk"])

    quant(T.uq[:], T.us[:], T.ut[:], ["ut"], ["uq"])
    op("a", lambda: S.activation(T.usr[:, 0:128], T.us[:, 0:128].indirect(T.ul[:, 0:8]), F.Copy), ["uq", "ul"], ["usr"])
    quant(T.bq[:, 192:320], T.bs[:, 192:320], T.bt1[:, 0:512], ["bz1"], ["bqz0"])
    scores(0, 0, False)
    op("v", lambda: V.tensor_copy(T.uqr[:, 0:128].bitcast(dt.uint32), T.uq[:, 0:128].bitcast(dt.uint32).indirect(T.ul[:, 0:8])), ["uq", "ul"], ["uqr"])
    act(T.dlt[:], T.aa[:], ["aa"], ["dlt"], func=F.Relu, bias=1.0, scale=-1.0)
    affine(T.iw[:], T.ci[:], 16.0, q1, ["ci", "qf"], ["iw"])
    affine(W["pbf"], T.ci[:], 1.0, K(0), ["ci", "k0"], ["pbf"])
    runs = ((0, min(EARLY)), (min(EARLY), max(EARLY) + 1), (max(EARLY) + 1, NV + 1), (NV + 1, NC))
    for i, (a, b) in enumerate(runs):
        later = sum(1 for c in range(b, NV + 1) if c not in EARLY)
        affine(T.kq[:, a:b], T.ci[:, a:b], 16.0 * (i % 2), 8.0 * later + (0 if i % 2 else 8.0 * (b - 1)), ["ci"], ["kr%d" % i])
    affine(T.kr[:], T.kq[:], 1.0, K(1), ["kr%d" % i for i in range(4)] + ["k1"], ["kr"])

    for i in (1, 2):
        affine(T["x%d" % i][:], T.eo[:, 0:3 * NC], 0.0, 0.0, ["eo"], ["xz%d" % i])

    def later_constants():
        affine(W["ahi"], T.iw[:], 1.0, C - 0.6, ["iw"], ["ahi"])
        affine(W["alo"], T.iw[:], 1.0, -0.5, ["iw"], ["alo"])
        affine(K(3), T.gf[:, 0:1], 1.0, q1, ["gf", "qf"], ["k3"])
        affine(T.x0[:], T.eo[:, 0:3 * NC], 0.0, 0.0, ["eo"], ["xz0"])
        affine(K(4), K(3), 0.5, -0.25, ["k3"], ["k4"])
        affine(K(5), K(4), 1.0, WHOLE, ["k4"], ["k5"])
        affine(T.wb[:, 16:16 + C], T.eo[:, 0:C], 0.0, float(C), ["eo"], ["wb_a"])
        affine(K(6), K(5), 1.0, -WHOLE, ["k5"], ["k6"])
        affine(T.wb[:, 0:16], T.eo[:, 0:16], 0.0, 0.0, ["eo"], ["wb_b"])
        affine(K(7), K(6), -2.0, K(3), ["k6", "k3"], ["k7"])
        affine(K(8), q1, 16.0, 0.0, ["qf"], ["k8"])
        affine(T.wb[:, 16 + C:32 + 2 * C], T.eo[:, 0:C + 16], 0.0, 0.0, ["eo"], ["wb"])
        affine(K(9), K(7), float(C + 16), K(8), ["k7", "k8"], ["k9"])

    def unit(t, b):
        if t == 0:
            quant(T.eq[:, 128 * b:128 * b + 128], T.es[:, 128 * b:128 * b + 128], T.ee[:, 3 - b:515 - b], ["ee"], ["eq%d" % b])

    def unpack(t):
        for b in range(4):
            k = ("ps3", "ps4", "ps0", "ps5")[b]
            mm(T[k][:, 0:C], T.eq[:, 128 * b:128 * b + 128], T.es[:, 128 * b:128 * b + 128], T["qp%d" % t][:], T["sp%d" % t][:], ["eq%d" % b, "qp%d" % t], [k])
            act(T.hw[:, 2 * C * b + C:2 * C * b + 2 * C], T[k][:, 0:C], [k], ["d%d" % b], scale=0.5)

    def turn(name, at):
        op("v", lambda: V.transpose(T[name][:, 0:C], T.wb[:, at + 16:at + 16 + C]), ["wb"], [name + "a"])
        op("v", lambda: V.transpose(T[name][:, C:C + E], T.wb[:, at:at + E]), ["wb", "wb_a", "wb_b"], [name + "b"])

    wlk = ["wl0", "wl1"]
    last = slice(15, C, 16)

    def pick(h):
        k = ("ps6", "ps3")[h]
        tt(T.m1[:, M * h:M * h + M], T[k][:, 0:M], T.mk[:, 0:M], A.min, [k, "mk"], ["m1_%d" % h])

    def hold(h):
        scan(T.exm[:, M * h:M * h + M], T.rs[:, 0:M], T.m1[:, M * h:M * h + M], [A.min, A.max], ["rs", "m1_%d" % h], ["exm%d" % h])

    for k in ("ps6", "ps2"):
        mm(T[k][:, 0:M], T.uqr[:], T.usr[:], T.qx0[:, 0:M], T.sx0[:, 0:M], ["uqr", "usr", "qx0_0"], [k])
    scores(0, 1)
    for t in range(ROUNDS):
        lw = T.x1[:, 2::3]
        if t == 0:
            op("gc_", lambda: g.affine_select(T.ee[:], T.eo[:], [[1, 516]], A.is_equal, 0.0, -3, -4), ["eo"], ["ee"])
            iota(T.iob[:], [[1, C]], -M, 0, "iob")

        def slot(c):
            k, at = ((c - 1) // 4, 0) if c > 4 else (1, 4 * 128)
            return T["bt%d" % k][:, at + (c - 1) % 4:at + 4 * 16 * c:4], "b%d" % c

        def own(c):
            return T.exm[:, 16 * c + 15:16 * c + 16], "exm%d" % (16 * c // M)

        def compare(c, bank):
            (o, k), (s, sk) = slot(c), own(c)
            ts(o, T[bank][:, 0:16 * c], s, -0.5, [A.is_lt, A.add], [bank, sk], [k])

        def rowsum(c):
            o, k = slot(c)
            act(T.fb[:, C * c:C * c + 16 * c], o, [k], ["acc%d" % c], accum=T.acc[:, c:c + 1])

        def sign(c):
            s, sk = own(c)
            bank = "ps2" if c in EARLY else "ps1"
            act(T.fb[:, C * c:C * c + 16 * c], T[bank][:, 0:16 * c], [bank, sk], ["sg%d" % c], scale=-1.0, bias=s, func=F.Sign)

        def relu(c):
            o, k = slot(c)
            act(o, T.fb[:, C * c:C * c + 16 * c], ["sg%d" % c], [k, "acc%d" % c], func=F.Relu, accum=T.acc[:, c:c + 1])

        def pack(k):
            at, n = SPAN[k][0], WIDTH[k]
            quant(T.bq[:, at:at + n], T.bs[:, at:at + n], T["bt%d" % k][:], ["b%d" % c for c in range(4 * k + 1 if k > 1 else 1, 4 * k + 5)] + ["bz%d" % k], ["bq%d" % k])

        def add(k):
            at, n = SPAN[k]
            mm(T.ps2[:, 0:n], T.oq[:], T.os_[:], T.bq[:, at:at + n], T.bs[:, at:at + n], ["oq", "bq%d" % max(k, 1), "bqz0", "bqz1"], ["ps2"], start=k == 0, stop=k == 2)

        def both(cs, bank):
            for c in cs:
                compare(c, bank)
                rowsum(c)

        if t == 0:
            quant(T.bq[:, 320:448], T.bs[:, 320:448], T.bt1[:, 0:512], ["bz1"], ["bqz1"])
            pick(0)
            cp(T.pbl[:], W["pbf"], ["pbf"], ["pbl"])
            hold(0)
        for step in (sign, relu):
            for c in EARLY:
                step(c)
        if t:
            both([4, 3, 2, 1, 7, 6], "ps6")
        pick(1)
        both([5], "ps6")
        hold(1)
        if t:
            pack(1)
        else:
            for c in (7, 6):
                compare(c, "ps6")
        for step in (sign, relu):
            for c in range(NC - 1, NV, -1):
                step(c)
        if t == 0:
            rowsum(7)
            rowsum(6)
            affine(T.iov[:], T.iof[:], 1.0 / C, 0.5 / C, ["iof"], ["iov"])
        tt(T.bt4[:, 3:4 * C:4], T.ps7[:, 0:C], T.exm[:], A.is_le, ["ps7", "exm0", "exm1", "bz4"], ["b20"])
        both(range(NV, 9, -1), "ps7")
        if t == 0:
            both([4, 3, 2, 1], "ps7")
            quant(T.oq[:], T.os_[:], T.bo[:], ["bo"], ["oq"])
            pack(1)
        for k in (3, 4, 2):
            pack(k)
        for k in (0, 1, 3, 4, 2):
            add(k)
        scan(T.sd[:], T.r0[:], T.bt4[:, 3:4 * C:4], [A.mult, A.add], ["r0", "b20"], ["sd"])
        if t == 0:
            tt(T.vb[:], T.pb[:].indirect(T.pbl[:]), T.iov[:], A.add, ["pb", "pbl", "iov"], ["vb"])
        tt(W["ab"], T.kr[:], T.sd[:, last], A.subtract, ["kr", "sd"], ["ab"])
        for j in (0, M):
            tt(T.ca[:, j:j + M], T.ps2[:, j:j + M], T.dlt[:, 0:M], A.mult, ["ps2", "dlt"], ["ca%d" % j])
        for j in (0, M):
            scan(T.cs[:, j:j + M], T.r0[:, 0:M], T.ca[:, j:j + M], [A.mult, A.add], ["r0", "ca%d" % j], ["cs%d" % j])
            if j == 0:
                tt(W["ac"], W["ab"], T.acc[:], A.subtract, ["ab"] + ["acc%d" % c for c in range(NC)], ["ac"])
        unit(t, 0)
        if t == 0:
            cp(lw, T.pin[:], ["pin", "xz1"], ["lw"])
            affine(W["kb"], lw, 1.0 / C, (1.0 - C) / C, ["lw"], ["kb"])
            later_constants()
        for dst, w, key in ((T.hw, 2 * C, "h"), (T.hx, C, "g")):
            for b in range(4):
                if t == 0:
                    act(dst[:, w * b:w * b + C], T.xt0[:, b:4 * C:4], ["xt_0", "xt_1"], [key + str(b)], scale=0.5)
                else:
                    act(dst[:, w * b:w * b + C], T.uu[:, C * b:C * b + C], ["uu%d_0" % b, "uu%d_1" % b], [key + str(b)], scale=2.0 ** -6)
        tt(W["pli"], W["ac"], T.cs[:, last], A.add, ["ac", "cs0", "cs%d" % M], ["pli"])
        unit(t, 1)
        pq = T.x2[:, 2::3]
        ts(W["hh"], W["pli"], -0.5, 0.5, [A.add, A.mult], ["pli"], ["hh"])
        ts(pq, W["pli"], -0.5, 0.25, [A.add, A.mult], ["pli", "xz2"], ["pq"])
        cp(T.plu[:], W["pli"], ["pli"], ["plu"])
        tt(W["pxi"], W["hh"], pq, A.subtract, ["hh", "pq"], ["pxi"])
        cp(T.wo[:].indirect(T.plu[:]), T.vb[:], ["plu", "vb"], ["wo"])
        ts(T.pxu[:], W["pxi"], 4.0, 0.5, [A.mult, A.add], ["pxi"], ["pxu"])
        tt(T.x2[:, 0::3], W["pxi"], pq, A.subtract, ["pxi", "pq"], ["dd"])
        affine(T.l4[:], T.wo[:], 1.0, WHOLE, ["wo"], ["l4"])
        affine(T.l5[:], T.l4[:], 1.0, -WHOLE, ["l4"], ["l5"])
        for j in (0, M):
            tt(T.gb[:, j:j + M], T.wo[:].indirect(T.pxu[:, j // 16:(j + M) // 16]), T.dlt[:, 0:M], A.mult, ["wo", "pxu", "dlt"], ["gb%d" % j])
        scan(T.gs[:, 0:M], T.r0[:, 0:M], T.gb[:, 0:M], [A.mult, A.add], ["r0", "gb0"], ["gs0"])
        scan(T.gs[:, M:C], T.r0[:, 0:M], T.gb[:, M:C], [A.mult, A.add], ["r0", "gb%d" % M], ["gs"])
        unit(t, 2)
        unit(t, 3)
        unpack(t)
        v = T.gs[:, last]
        tt(W["lb"], v, W["ahi"], A.min, ["gs", "ahi"], ["lb"])
        tt(W["yi"], v, W["kb"], A.subtract, ["gs", "kb"], ["yi"])
        tt(T.x0[:, 1::3], v, W["alo"], A.is_ge, ["gs", "alo", "xz0"], ["o1"])
        tt(T.x1[:, 0::3], v, lw, A.subtract, ["gs", "lw"], ["dl"])
        tt(T.x0[:, 2::3], W["yi"], W["lb"], A.is_equal, ["yi", "lb"], ["o34"])
        if t == 0:
            cp(T.wl[:, 0:1], K(9), ["k9"], ["wl0"])
            ts(T.wl[:, 1:2], K(9), 256.0, float(C + E - 1), [A.add, A.min], ["k9"], ["wl1"])
        scan(T.y1[:], T.x0[:], T.x1[:], [A.mult, A.add], ["o1", "o34", "dl", "lw"], ["y1"])
        scan(T.y2[:], T.x0[:], T.x2[:], [A.mult, A.add], ["o1", "o34", "dd", "pq"], ["y2"])
        ts(T.lu[:], T.y1[:, 2::3], WHOLE, -WHOLE, [A.add, A.add], ["y1"], ["lu"])
        ts(T.pu[:], T.y2[:, 2::3], 4.0, 0.5, [A.mult, A.add], ["y2"], ["pu"])
        if t + 1 < ROUNDS:
            affine(W["lr"], T.y1[:, 2::3], 1.0, WHOLE, ["y1"], ["lr"])
            affine(lw, W["lr"], 1.0, -WHOLE, ["lr"], ["lw"])
            affine(W["kb"], lw, 1.0 / C, (1.0 - C) / C, ["lw"], ["kb"])
        cp(T.wb[:, 16:16 + 2 * C].indirect(T.lu[:]), T.iob[:], ["lu", "iob", "wb_a"], ["wb"])
        turn("tu", C)
        up = "up%d" % t
        cp(T[up][:], T.tu[:].indirect(T.wl[:]), ["tua", "tub"] + wlk, [up])
        send(T["la%d" % t][:], T[up][:, 0:NC], "rl%d" % t, "ll%d" % t, [up])
        turn("tl", 0)
        if t + 1 < ROUNDS:
            tt(T.vb[:], T.l5[:].indirect(T.pu[:]), T.iov[:], A.add, ["l5", "pu", "iov"], ["vb"])
        else:
            act(T.olb[:], T.l5[:].indirect(T.pu[:]), ["l5", "pu"], ["olb"])
            dma("s", T.ol[:], T.olb[0:128:16, :], "dol", ["olb"], [])
            quant(T.vq[:], T.vs[:], T.vt[:], ["vt"], ["vq"])
        ts(T.lo[:], T.tl[:].indirect(T.wl[:]), float(M), None, [A.add], ["tla", "tlb"] + wlk, ["lo"])
        tt(T.ef[:], T.lo[:, 0:NC], T["la%d" % t][:], A.add, ["lo", "la%d" % t], ["ef"])
        cp(T.eu[:], T.ef[:], ["ef"], ["eu"])
        banks = (("ps6", "ps7", "ps1", "ps2"), ("ps3", "ps4", "ps0", "ps5"))

        def blend(b, h, n):
            o, j, w = 2 * C * b, M * h, M * n
            zk = ["z%d_%d" % (b, i) for i in range(h, h + n)]
            tt(T.z[:, 4 * j + b:4 * (j + w):4], T.hw[:, o:o + 2 * C].indirect(T.eu[:, j // 16:(j + w) // 16]), T.hx[:, C * b + j:C * b + j + w], A.add,
               ["eu", "h%d" % b, "g%d" % b, "d%d" % b], zk)
            act(T.z32[:, C * b + j:C * b + j + w], T.z[:, 4 * j + b:4 * (j + w):4], zk, ["zz%d_%d" % (b, i) for i in range(h, h + n)], scale=32.0)

        def layer(h):
            j = M * h
            quant(T.zq[:, j:j + M], T.zs[:, j:j + M], T.z[:, 4 * j:4 * (j + M)], ["z%d_%d" % (b, h) for b in range(4)], ["zq%d" % h])
            for b in range(4):
                k = banks[h][b]
                mm(T[k][:, 0:M], T.wq[:, 128 * b:128 * b + 128], T.wp[:, 128 * b:128 * b + 128], T.zq[:, j:j + M], T.zs[:, j:j + M], ["w", "zq%d" % h], [k])

        def state(b, h, scaled=True):
            j = M * h
            k, u = banks[h][b], T.uu[:, C * b + j:C * b + j + M]
            tt(u, T[k][:, 0:M], T.z32[:, C * b + j:C * b + j + M], A.add, [k, "zz%d_%d" % (b, h)], ["uu%d_%d" % (b, h)])
            if b < 3 and scaled:
                act(T.xt1[:, 4 * j + b:4 * (j + M):4], u, ["uu%d_%d" % (b, h)], ["x%d_%d" % (b, h)], scale=2.0 ** -5)

        def quarter(h, b=3):
            j = M * h
            ts(T.xt1[:, 4 * j + b:4 * (j + M):4], T.uu[:, b * C + j:b * C + j + M], 2.0 ** -5, None, [A.mult], ["uu%d_%d" % (b, h)], ["x%d_%d" % (b, h)])

        for b, h, n in ((0, 0, 2), (1, 0, 1), (2, 0, 1), (3, 0, 1), (1, 1, 1)):
            blend(b, h, n)
        layer(0)
        blend(2, 1, 1)
        blend(3, 1, 1)
        state(0, 0)
        layer(1)
        for b, h in ((1, 0), (2, 0), (3, 0), (0, 1)):
            state(b, h)
        quarter(0)
        state(1, 1)
        scores(t + 1, 0)
        if t + 1 < ROUNDS:
            state(2, 1)
            state(3, 1)
            pick(0)
            quarter(1)
            hold(0)
        else:
            state(2, 1, False)
            state(3, 1)
            quarter(1, 2)
            quarter(1)
            act(T.yb[:, 0:M], T.ps6[:, 0:M], ["ps6"], ["yb0"])
            dma("a", T.y[:, 0:M], T.yb[:, 0:M], "dy", ["yb0"], [])
        scores(t + 1, 1)

    cp(T.yb[:, M:C], T.ps7[:, 0:M], ["ps7"], ["yb1"])
    for k in range(4):
        dma("s", T.osc[4 * k:4 * k + 4, :], T.sx3[32 * k:32 * k + 4, :], "doc", ["qx3_0", "qx3_1"], [])
    dma("a", T.y[:, M:C], T.yb[:, M:C], "dy", ["yb1"], [])
    for t in range(ROUNDS):
        count["rq%d" % t], count["rl%d" % t] = 2 * nmask, nmask
    need("s", [(s, m) for s, m in count.items()])
